import numpy as np
import ml_dtypes


def mxq(x, axis, fmt="e4m3"):
    dtype, down = {"e4m3": (ml_dtypes.float8_e4m3fn, 7), "e5m2": (ml_dtypes.float8_e5m2, 14)}[fmt]
    v = np.moveaxis(np.asarray(x, np.float32).astype(ml_dtypes.bfloat16).astype(np.float64), axis, -1)
    blocks = v.reshape(v.shape[:-1] + (-1, 32))
    amax = np.abs(blocks).max(-1, keepdims=True)
    byte = np.maximum(np.where(amax > 0, np.frexp(amax)[1] - 1 + 127, 0) - down, 1)
    scale = np.exp2(byte - 127.0)
    codes = (blocks / scale).astype(np.float32).astype(dtype).astype(np.float64)
    return np.moveaxis((codes * scale).reshape(v.shape), -1, axis)


WIDE = False


def mx_kscale(k):
    if not WIDE:
        return np.ones(k)
    levels = np.array([10, -10, 5, -5, 0])
    if k % 512:
        return np.exp2(np.random.permutation(np.resize(levels, k // 32))).repeat(32)
    a = np.empty((k // 512, 16))
    for p in range(k // 512):
        a[p, :8] = np.random.permutation(np.resize(levels, 8))
        for g in range(8):
            far = levels[np.abs(levels - a[p, g]) >= 10]
            a[p, g + 8] = far[np.random.randint(len(far))]
    return np.exp2(a.ravel()).repeat(32)


def f64(x):
    return np.asarray(x).astype(np.float64)


def striped(idx):
    return np.tile(idx.reshape(-1, 16).T, (8, 1)).astype(np.uint16)


def unstriped(offs):
    return offs[:16].T.reshape(-1).astype(np.int64)


E2M1 = np.array([0.0, 0.5, 1.0, 1.5, 2.0, 3.0, 4.0, 6.0, -0.0, -0.5, -1.0, -1.5, -2.0, -3.0, -4.0, -6.0])


def pack_weight(w, fmt):
    k, n = w.shape
    w = f64(np.asarray(w, np.float32).astype(ml_dtypes.bfloat16)).reshape(k // 32, 32, n)
    amax = np.abs(w).max(1)
    if fmt == "e4m3":
        byte = np.frexp(amax)[1] - 1 + 127 - 7
    else:
        mant, ex = np.frexp(amax / 6.0)
        byte = np.where(mant > 0.5, ex, ex - 1) + 127
    byte = np.clip(np.where(amax > 0, byte, 1), 1, 254)
    scaled = (w * np.exp2(127.0 - byte)[:, None, :]).reshape(k, n).astype(np.float32)
    by_word = np.ascontiguousarray(scaled.reshape(k // 512, 128, 4, n).transpose(0, 1, 3, 2))
    if fmt == "e4m3":
        words = by_word.astype(ml_dtypes.float8_e4m3fn).view(np.uint8)
    else:
        c = by_word.astype(ml_dtypes.float4_e2m1fn).view(np.uint8) & 0xF
        words = (c[..., 0::2] | (c[..., 1::2] << 4)).reshape(k // 512, 128, 2 * n)
    return np.ascontiguousarray(words), np.ascontiguousarray(byte.astype(np.uint8).reshape(k // 512, 16, n))


def unpack_weight(words, scales, fmt):
    g, _, n = scales.shape
    words = np.ascontiguousarray(words).reshape(g, 128, n, -1)
    if fmt == "e4m3":
        vals = words.view(ml_dtypes.float8_e4m3fn).astype(np.float64)
    else:
        nib = np.empty((g, 128, n, 4), np.uint8)
        nib[..., 0::2] = words & 0xF
        nib[..., 1::2] = words >> 4
        vals = E2M1[nib]
    vals = vals * np.repeat(np.exp2(scales.astype(np.float64) - 127.0), 8, axis=1)[..., None]
    return vals.transpose(0, 1, 3, 2).reshape(g * 512, n)


def silu(v):
    return v / (1.0 + np.exp(-np.maximum(v, -700.0)))


K, T, E, N = 2048, 768, 2, 384
COUNTS = (256, 512)
STARTS = np.cumsum((0,) + COUNTS)


def by_expert(wq, xq):
    return np.concatenate([wq[e].T @ xq[:, STARTS[e]:STARTS[e + 1]] for e in range(E)], axis=1)


def setup_inputs():
    n = np.random.standard_normal
    s = mx_kscale(K)[:, None]
    expert = np.random.permutation(np.repeat(np.arange(E), COUNTS))
    slot_token = np.argsort(expert, kind="stable")
    w = [pack_weight(m, "e2m1") for m in n((E, K, N)) / np.sqrt(K) / s[None]]
    return {
        "xT": (n((K, T)) * s).astype(np.float32),
        "w_words": np.stack([m[0] for m in w]),
        "w_scales": np.stack([m[1] for m in w]),
        "b": (0.3 * n((N, E))).astype(np.float32),
        "gate": np.tile(np.random.uniform(0.2, 1.0, T), (N, 1)).astype(np.float32),
        "offs": striped(slot_token),
    }


def reference(xT, w_words, w_scales, b, gate, offs):
    idx = unstriped(offs)
    w = np.stack([unpack_weight(w_words[e], w_scales[e], "e2m1") for e in range(E)])
    xq = mxq(f64(xT)[:, idx], 0, "e4m3")
    y = by_expert(w, xq)
    y = silu(y + np.repeat(f64(b), COUNTS, axis=1))
    out = np.zeros((N, T))
    out[:, idx] = f64(gate) * y
    return out

@@ -1,0 +1,213 @@
+import concourse.mybir as mybir
+
+K, T, E, N = 2048, 768, 2, 384
+COUNTS = (256, 512)
+STARTS = (0, 256)
+FLOPS = 2 * T * K * N
+
+P = 128
+PACK = 4
+K_PASS = P * PACK
+PASSES = K // K_PASS
+N_BLOCKS = N // P
+WINDOW = 1024
+
+F32 = mybir.dt.float32
+BF16 = mybir.dt.bfloat16
+I32 = mybir.dt.int32
+U32 = mybir.dt.uint32
+U16 = mybir.dt.uint16
+U8 = mybir.dt.uint8
+E4M3X4 = mybir.dt.float8_e4m3fn_x4
+E2M1X4 = mybir.dt.float4_e2m1fn_x4
+COPY = mybir.ActivationFunctionType.Copy
+SILU = mybir.ActivationFunctionType.Silu
+MULT = mybir.AluOpType.mult
+
+
+def tile_moe_rag_lin_silu_kernel(tc, xT, w_words, w_scales, b, gate, offs, out):
+    nc = tc.nc
+    with tc.tile_pool(name="keep", bufs=1) as keep, tc.psum_pool(name="psum", bufs=1) as psum:
+        offsets = keep.tile([P, T // 16], U16, name="offsets")
+        raw = [keep.tile([P, PACK, T], F32, name="raw%d" % a, align_bytes=64) for a in range(PASSES)]
+        grouped = [keep.tile([P, T, PACK], BF16, name="grouped%d" % a, align_bytes=64) for a in range(PASSES)]
+        words = keep.tile([P, PASSES, WINDOW], I32, name="words", align_bytes=64)
+        scales = keep.tile([P, PASSES, WINDOW], U8, name="scales", align_bytes=64)
+        slot_words = [keep.tile([P, T], U32, name="slot_words%d" % a, align_bytes=64) for a in range(PASSES)]
+        slot_scales = [keep.tile([P, T], U8, name="slot_scales%d" % a, align_bytes=64) for a in range(PASSES)]
+        w_codes = [keep.tile([P, E, 2 * N], U8, name="w_codes%d" % a, align_bytes=64) for a in range(PASSES)]
+        w_planes = keep.tile([P, E * PASSES, N], U8, name="w_planes", align_bytes=64)
+        bias = keep.tile([P, N_BLOCKS, E], F32, name="bias")
+        gates = keep.tile([P, N_BLOCKS, T], F32, name="gates")
+        probe = keep.tile([P, 1], F32, name="probe")
+        y = [keep.tile([P, T], F32, name="y%d" % n) for n in range(N_BLOCKS)]
+        gy = [keep.tile([P, T], F32, name="gy%d" % n) for n in range(N_BLOCKS)]
+        spread = [keep.tile([P, WINDOW], F32, name="spread%d" % n) for n in range(N_BLOCKS)]
+        acc0 = [psum.tile([P, COUNTS[0]], F32, name="acc0_%d" % n) for n in range(N_BLOCKS)]
+        acc1 = [psum.tile([P, COUNTS[1]], F32, name="acc1_%d" % n) for n in range(N_BLOCKS)]
+
+        def load_x(a, t0, t1):
+            rows = xT[a * K_PASS : (a + 1) * K_PASS, :].rearrange("(p j) w -> p j w", j=PACK)
+            nc.sync.dma_start(out=raw[a][:, :, t0:t1], in_=rows[:, :, t0:t1])
+
+        def load_w(a):
+            nc.sync.dma_start(
+                out=w_codes[a][:].bitcast(I32),
+                in_=w_words[:, a].rearrange("e p c -> p e c").bitcast(I32),
+            )
+
+        def load_offs():
+            nc.sync.dma_start(offsets[:], offs)
+
+        def load_gate(n):
+            nc.sync.dma_start(out=gates[:, n, :], in_=gate[P * n : P * (n + 1), :])
+
+        nc.vector.memset(probe[:], 0.0)
+        nc.scalar.activation(probe[:], probe[:], SILU)
+        planes = w_planes[:].rearrange("p g n -> p (g n)").bitcast(I32)
+        nc.vector.memset(planes, 0)
+        nc.gpsimd.memset(scales[:].rearrange("p a t -> p (a t)").bitcast(I32), 0)
+        nc.vector.memset(words[:, :, T:WINDOW], 0)
+        for quadrant in range(4):
+            nc.scalar.dma_start(
+                out=planes[32 * quadrant : 32 * quadrant + 4, :].rearrange("r (g n) -> r g n", g=E * PASSES),
+                in_=w_scales[:, :, 4 * quadrant : 4 * quadrant + 4, :].rearrange("e a r n -> r (e a) n").bitcast(I32),
+            )
+        nc.scalar.dma_start(out=bias[:], in_=b.rearrange("(c p) e -> p c e", p=P))
+
+        load_x(0, 0, 768)
+        load_offs()
+        load_x(1, 0, 768)
+        load_x(2, 0, 768)
+        load_w(0)
+        load_x(3, 0, 512)
+        load_x(3, 512, 768)
+        load_w(1)
+        load_w(2)
+        load_w(3)
+        load_gate(0)
+        load_gate(1)
+        load_gate(2)
+
+        def cast_v(a, t0, t1):
+            dst = grouped[a][:, t0:t1, :].rearrange("p (c i) j -> p c j i", i=4)
+            src = raw[a][:, :, t0:t1].rearrange("p j (c i) -> p c j i", i=4)
+            nc.vector.tensor_copy(dst, src)
+
+        def cast_s(a, t0, t1):
+            dst = grouped[a][:, t0:t1, :].rearrange("p (c i) j -> p c j i", i=4)
+            src = raw[a][:, :, t0:t1].rearrange("p j (c i) -> p c j i", i=4)
+            nc.scalar.activation(dst, src, COPY)
+
+        def quantize(a, t0, t1):
+            nc.vector.quantize_mx(
+                out=words[:, a, t0:t1].bitcast(E4M3X4),
+                scales=scales[:, a, t0:t1],
+                in_=grouped[a][:, t0:t1, :].rearrange("p t j -> p (t j)"),
+            )
+
+        def gather_words(a, s0, s1):
+            nc.vector.tensor_copy(
+                slot_words[a][:, s0:s1], words[:, a, :].bitcast(U32).indirect(offsets[:, s0 // 16 : s1 // 16])
+            )
+
+        def gather_bytes(a, s0, s1):
+            nc.vector.tensor_copy(slot_scales[a][:, s0:s1], scales[:, a, :].indirect(offsets[:, s0 // 16 : s1 // 16]))
+
+        def multiply(a, e, n, s0, s1, acc):
+            nc.tensor.matmul_mx(
+                out=acc,
+                lhsT=w_codes[a][:, e, 2 * P * n : 2 * P * (n + 1)].bitcast(E2M1X4),
+                lhsT_scale=w_planes[:, e * PASSES + a, P * n : P * (n + 1)],
+                rhs=slot_words[a][:, s0:s1].bitcast(E4M3X4),
+                rhs_scale=slot_scales[a][:, s0:s1],
+                start=(a == 0),
+                stop=(a == PASSES - 1),
+            )
+
+        def mm1(a):
+            for n in range(N_BLOCKS):
+                multiply(a, 1, n, 256, 768, acc1[n][:])
+
+        def mm0(a):
+            for n in range(N_BLOCKS):
+                multiply(a, 0, n, 0, 128, acc0[n][:, 0:128])
+
+        def mm0_last(n):
+            multiply(PASSES - 1, 0, n, 0, 128, acc0[n][:, 0:128])
+            for a in range(PASSES):
+                multiply(a, 0, n, 128, 256, acc0[n][:, 128:256])
+
+        def activate(e, n):
+            s0, s1 = STARTS[e], STARTS[e] + COUNTS[e]
+            acc = (acc0, acc1)[e][n]
+            nc.scalar.activation(y[n][:, s0:s1], acc[:], SILU, bias=bias[:, n, e : e + 1])
+
+        def scatter(n, s0, s1):
+            nc.vector.tensor_tensor(
+                spread[n][:].indirect(offsets[:, s0 // 16 : s1 // 16]), y[n][:, s0:s1], gates[:, n, s0:s1], MULT
+            )
+
+        def mult_v(n, s0, s1):
+            nc.vector.tensor_tensor(gy[n][:, s0:s1], y[n][:, s0:s1], gates[:, n, s0:s1], MULT)
+
+        def mult_g(n, s0, s1):
+            nc.gpsimd.tensor_tensor(gy[n][:, s0:s1], y[n][:, s0:s1], gates[:, n, s0:s1], MULT)
+
+        def scatter_copy(n, s0, s1):
+            nc.vector.tensor_copy(spread[n][:].indirect(offsets[:, s0 // 16 : s1 // 16]), gy[n][:, s0:s1])
+
+        def store(n):
+            nc.sync.dma_start(out=out[P * n : P * (n + 1), :], in_=spread[n][:, 0:T])
+
+        cast_v(0, 0, 384)
+        cast_s(0, 384, 512)
+        cast_s(0, 512, 768)
+        quantize(0, 0, 512)
+        quantize(0, 512, 768)
+        gather_words(0, 0, 768)
+        cast_v(1, 0, 256)
+        cast_s(1, 256, 512)
+        cast_s(1, 512, 768)
+        gather_bytes(0, 0, 768)
+        mm1(0)
+        mm0(0)
+        quantize(1, 0, 512)
+        quantize(1, 512, 768)
+        gather_words(1, 0, 768)
+        cast_v(2, 0, 128)
+        cast_s(2, 128, 512)
+        cast_s(2, 512, 768)
+        gather_bytes(1, 0, 768)
+        mm1(1)
+        mm0(1)
+        quantize(2, 0, 512)
+        quantize(2, 512, 768)
+        gather_words(2, 0, 768)
+        gather_bytes(2, 0, 768)
+        mm1(2)
+        mm0(2)
+        cast_s(3, 0, 256)
+        cast_s(3, 256, 512)
+        cast_s(3, 512, 768)
+        quantize(3, 0, 512)
+        quantize(3, 512, 768)
+        gather_words(3, 0, 256)
+        gather_bytes(3, 0, 256)
+        for n in range(N_BLOCKS):
+            mm0_last(n)
+            activate(0, n)
+        gather_words(3, 256, 768)
+        gather_bytes(3, 256, 768)
+        mm1(3)
+        for n in range(N_BLOCKS):
+            activate(1, n)
+        scatter(0, 0, 256)
+        scatter(1, 0, 256)
+        scatter(0, 256, 768)
+        store(0)
+        scatter(2, 0, 256)
+        scatter(1, 256, 768)
+        store(1)
+        scatter(2, 256, 768)
+        store(2)

@@ -1,16 +1,20 @@
 import concourse.mybir as mybir
 
 K, T, E, N = 2048, 768, 2, 384
-COUNTS = (256, 512)
-STARTS = (0, 256)
 FLOPS = 2 * T * K * N
+BYTES = 4 * K * T + E * K * N // 2 + E * K * N // 32 + 4 * N * E + 4 * T + 2 * T + 4 * N * T
 
 P = 128
 PACK = 4
 K_PASS = P * PACK
 PASSES = K // K_PASS
+LAST = PASSES - 1
 N_BLOCKS = N // P
-WINDOW = 1024
+PIECE = 256
+EARLY = 512
+WIDE = 1024
+PACKED = (0,1,2)
+VECTOR_FROM = (384, 384)
 
 F32 = mybir.dt.float32
 BF16 = mybir.dt.bfloat16
@@ -24,190 +28,195 @@ COPY = mybir.ActivationFunctionType.Copy
 SILU = mybir.ActivationFunctionType.Silu
 MULT = mybir.AluOpType.mult
 
+PART_A = (256, 1, EARLY)
+PART_B = (512, 1, T)
+PART_C = (0, 0, T)
+PARTS = (PART_A, PART_B, PART_C)
+
 
 def tile_moe_rag_lin_silu_kernel(tc, xT, w_words, w_scales, b, gate, offs, out):
     nc = tc.nc
     with tc.tile_pool(name="keep", bufs=1) as keep, tc.psum_pool(name="psum", bufs=1) as psum:
         offsets = keep.tile([P, T // 16], U16, name="offsets")
-        raw = [keep.tile([P, PACK, T], F32, name="raw%d" % a, align_bytes=64) for a in range(PASSES)]
+        raw = [keep.tile([P, PACK, T], F32, name="raw%d" % a, align_bytes=64) for a in range(LAST)]
+        raw_early = keep.tile([P, PACK, EARLY], F32, name="raw_early", align_bytes=64)
+        raw_late = keep.tile([P, PACK, T - EARLY], F32, name="raw_late", align_bytes=64)
         grouped = [keep.tile([P, T, PACK], BF16, name="grouped%d" % a, align_bytes=64) for a in range(PASSES)]
-        words = keep.tile([P, PASSES, WINDOW], I32, name="words", align_bytes=64)
-        scales = keep.tile([P, PASSES, WINDOW], U8, name="scales", align_bytes=64)
+        words = [keep.tile([P, T], I32, name="words%d" % a, align_bytes=64) for a in range(PASSES)]
+        scales = {}
+        slot_scales = {}
+        for a in range(PASSES):
+            if a not in PACKED[1:]:
+                scales[a] = keep.tile([P, WIDE], U8, name="scales%d" % a, align_bytes=64)
+            slot_scales[a] = keep.tile([P, T], U8, name="slot_scales%d" % a, align_bytes=64)
         slot_words = [keep.tile([P, T], U32, name="slot_words%d" % a, align_bytes=64) for a in range(PASSES)]
-        slot_scales = [keep.tile([P, T], U8, name="slot_scales%d" % a, align_bytes=64) for a in range(PASSES)]
-        w_codes = [keep.tile([P, E, 2 * N], U8, name="w_codes%d" % a, align_bytes=64) for a in range(PASSES)]
+        w_codes = [keep.tile([P, PASSES, 2 * N], U8, name="w_codes%d" % e, align_bytes=64) for e in range(E)]
         w_planes = keep.tile([P, E * PASSES, N], U8, name="w_planes", align_bytes=64)
         bias = keep.tile([P, N_BLOCKS, E], F32, name="bias")
-        gates = keep.tile([P, N_BLOCKS, T], F32, name="gates")
+        gates = [keep.tile([P, PIECE * (e + 1)], F32, name="gates%d" % e) for e in range(E)]
         probe = keep.tile([P, 1], F32, name="probe")
         y = [keep.tile([P, T], F32, name="y%d" % n) for n in range(N_BLOCKS)]
-        gy = [keep.tile([P, T], F32, name="gy%d" % n) for n in range(N_BLOCKS)]
-        spread = [keep.tile([P, WINDOW], F32, name="spread%d" % n) for n in range(N_BLOCKS)]
-        acc0 = [psum.tile([P, COUNTS[0]], F32, name="acc0_%d" % n) for n in range(N_BLOCKS)]
-        acc1 = [psum.tile([P, COUNTS[1]], F32, name="acc1_%d" % n) for n in range(N_BLOCKS)]
+        spread = [keep.tile([P, T], F32, name="spread%d" % n) for n in range(N_BLOCKS)]
+        banks = [psum.tile([P, 512], F32, name="bank%d" % i) for i in range(8)]
 
-        def load_x(a, t0, t1):
-            rows = xT[a * K_PASS : (a + 1) * K_PASS, :].rearrange("(p j) w -> p j w", j=PACK)
-            nc.sync.dma_start(out=raw[a][:, :, t0:t1], in_=rows[:, :, t0:t1])
+        def x_rows(a):
+            return xT[a * K_PASS : (a + 1) * K_PASS, :].rearrange("(p j) w -> p j w", j=PACK)
 
-        def load_w(a):
+        def load_w(e):
             nc.sync.dma_start(
-                out=w_codes[a][:].bitcast(I32),
-                in_=w_words[:, a].rearrange("e p c -> p e c").bitcast(I32),
+                out=w_codes[e][:].bitcast(I32), in_=w_words[e].rearrange("a p c -> p a c").bitcast(I32)
             )
-
-        def load_offs():
-            nc.sync.dma_start(offsets[:], offs)
-
-        def load_gate(n):
-            nc.sync.dma_start(out=gates[:, n, :], in_=gate[P * n : P * (n + 1), :])
 
         nc.vector.memset(probe[:], 0.0)
         nc.scalar.activation(probe[:], probe[:], SILU)
         planes = w_planes[:].rearrange("p g n -> p (g n)").bitcast(I32)
         nc.vector.memset(planes, 0)
-        nc.gpsimd.memset(scales[:].rearrange("p a t -> p (a t)").bitcast(I32), 0)
-        nc.vector.memset(words[:, :, T:WINDOW], 0)
+        for a in scales:
+            nc.vector.memset(scales[a][:].bitcast(I32), 0)
+        for a in PACKED[1:]:
+            nc.vector.memset(slot_scales[a][:].bitcast(I32), 0)
+
+        nc.sync.dma_start(out=raw[0][:], in_=x_rows(0))
+        nc.sync.dma_start(offsets[:], offs)
+        for a in range(1, LAST):
+            nc.sync.dma_start(out=raw[a][:], in_=x_rows(a))
+        nc.sync.dma_start(out=raw_early[:], in_=x_rows(LAST)[:, :, 0:EARLY])
+        nc.sync.dma_start(out=raw_late[:], in_=x_rows(LAST)[:, :, EARLY:T])
         for quadrant in range(4):
-            nc.scalar.dma_start(
+            nc.sync.dma_start(
                 out=planes[32 * quadrant : 32 * quadrant + 4, :].rearrange("r (g n) -> r g n", g=E * PASSES),
                 in_=w_scales[:, :, 4 * quadrant : 4 * quadrant + 4, :].rearrange("e a r n -> r (e a) n").bitcast(I32),
             )
-        nc.scalar.dma_start(out=bias[:], in_=b.rearrange("(c p) e -> p c e", p=P))
-
-        load_x(0, 0, 768)
-        load_offs()
-        load_x(1, 0, 768)
-        load_x(2, 0, 768)
-        load_w(0)
-        load_x(3, 0, 512)
-        load_x(3, 512, 768)
         load_w(1)
-        load_w(2)
-        load_w(3)
-        load_gate(0)
-        load_gate(1)
-        load_gate(2)
 
-        def cast_v(a, t0, t1):
-            dst = grouped[a][:, t0:t1, :].rearrange("p (c i) j -> p c j i", i=4)
-            src = raw[a][:, :, t0:t1].rearrange("p j (c i) -> p c j i", i=4)
-            nc.vector.tensor_copy(dst, src)
+        def late_loads():
+            nc.sync.dma_start(out=bias[:], in_=b.rearrange("(c p) e -> p c e", p=P))
+            nc.sync.dma_start(out=gates[1][:], in_=gate[0:P, PIECE:T])
+            load_w(0)
+            nc.sync.dma_start(out=gates[0][:], in_=gate[0:P, 0:PIECE])
 
-        def cast_s(a, t0, t1):
+        def cast(engine, a, t0, t1):
+            if a < LAST:
+                src = raw[a][:, :, t0:t1]
+            elif t0 < EARLY:
+                src = raw_early[:, :, t0:t1]
+            else:
+                src = raw_late[:, :, t0 - EARLY : t1 - EARLY]
             dst = grouped[a][:, t0:t1, :].rearrange("p (c i) j -> p c j i", i=4)
-            src = raw[a][:, :, t0:t1].rearrange("p j (c i) -> p c j i", i=4)
-            nc.scalar.activation(dst, src, COPY)
+            src = src.rearrange("p j (c i) -> p c j i", i=4)
+            if engine == "vector":
+                nc.vector.tensor_copy(dst, src)
+            else:
+                nc.scalar.activation(dst, src, COPY)
 
         def quantize(a, t0, t1):
+            if a in PACKED:
+                plane = scales[PACKED[0]][4 * PACKED.index(a) : P, t0:t1]
+            else:
+                plane = scales[a][:, t0:t1]
             nc.vector.quantize_mx(
-                out=words[:, a, t0:t1].bitcast(E4M3X4),
-                scales=scales[:, a, t0:t1],
+                out=words[a][:, t0:t1].bitcast(E4M3X4),
+                scales=plane,
                 in_=grouped[a][:, t0:t1, :].rearrange("p t j -> p (t j)"),
             )
 
-        def gather_words(a, s0, s1):
+        def entries(s0, s1):
+            return offsets[:, s0 // 16 : s1 // 16]
+
+        def gather_words(a, part):
+            s0, e, width = part
             nc.vector.tensor_copy(
-                slot_words[a][:, s0:s1], words[:, a, :].bitcast(U32).indirect(offsets[:, s0 // 16 : s1 // 16])
+                slot_words[a][:, s0 : s0 + PIECE], words[a][:, 0:width].bitcast(U32).indirect(entries(s0, s0 + PIECE))
             )
 
-        def gather_bytes(a, s0, s1):
-            nc.vector.tensor_copy(slot_scales[a][:, s0:s1], scales[:, a, :].indirect(offsets[:, s0 // 16 : s1 // 16]))
+        def gather_bytes(a, s0, s1, width):
+            nc.vector.tensor_copy(slot_scales[a][:, s0:s1], scales[a][:, 0:width].indirect(entries(s0, s1)))
 
-        def multiply(a, e, n, s0, s1, acc):
+        def shift(a):
+            first = 4 * PACKED.index(a)
+            nc.sync.dma_start(
+                out=slot_scales[a][0:112, :].bitcast(I32),
+                in_=slot_scales[PACKED[0]][first : first + 112, :].bitcast(I32),
+            )
+
+        groups = [(n, PART_A, h) for n in range(N_BLOCKS) for h in range(2)]
+        groups = groups + [(n, part, h) for n in range(N_BLOCKS) for part in (PART_B, PART_C) for h in range(2)]
+
+        def acc(g):
+            late = g - 6
+            bank, turn = (g, 0) if g < 8 else ((late - 2) % 8, 1 + (late - 2) // 8)
+            return banks[bank][:, P * turn : P * (turn + 1)]
+
+        def multiply(a, g):
+            n, part, h = groups[g]
+            s0 = part[0] + P * h
+            e = part[1]
             nc.tensor.matmul_mx(
-                out=acc,
-                lhsT=w_codes[a][:, e, 2 * P * n : 2 * P * (n + 1)].bitcast(E2M1X4),
+                out=acc(g),
+                lhsT=w_codes[e][:, a, 2 * P * n : 2 * P * (n + 1)].bitcast(E2M1X4),
                 lhsT_scale=w_planes[:, e * PASSES + a, P * n : P * (n + 1)],
-                rhs=slot_words[a][:, s0:s1].bitcast(E4M3X4),
-                rhs_scale=slot_scales[a][:, s0:s1],
+                rhs=slot_words[a][:, s0 : s0 + P].bitcast(E4M3X4),
+                rhs_scale=slot_scales[a][:, s0 : s0 + P],
                 start=(a == 0),
-                stop=(a == PASSES - 1),
+                stop=(a == LAST),
             )
 
-        def mm1(a):
-            for n in range(N_BLOCKS):
-                multiply(a, 1, n, 256, 768, acc1[n][:])
+        def activate(g):
+            n, part, h = groups[g]
+            s0 = part[0] + P * h
+            e = part[1]
+            nc.scalar.activation(y[n][:, s0 : s0 + P], acc(g), SILU, bias=bias[:, n, e : e + 1])
 
-        def mm0(a):
-            for n in range(N_BLOCKS):
-                multiply(a, 0, n, 0, 128, acc0[n][:, 0:128])
-
-        def mm0_last(n):
-            multiply(PASSES - 1, 0, n, 0, 128, acc0[n][:, 0:128])
-            for a in range(PASSES):
-                multiply(a, 0, n, 128, 256, acc0[n][:, 128:256])
-
-        def activate(e, n):
-            s0, s1 = STARTS[e], STARTS[e] + COUNTS[e]
-            acc = (acc0, acc1)[e][n]
-            nc.scalar.activation(y[n][:, s0:s1], acc[:], SILU, bias=bias[:, n, e : e + 1])
-
-        def scatter(n, s0, s1):
+        def scatter(n, part):
+            s0, e, width = part
+            g0 = s0 - PIECE * e
             nc.vector.tensor_tensor(
-                spread[n][:].indirect(offsets[:, s0 // 16 : s1 // 16]), y[n][:, s0:s1], gates[:, n, s0:s1], MULT
+                spread[n][:].indirect(entries(s0, s0 + PIECE)),
+                y[n][:, s0 : s0 + PIECE],
+                gates[e][:, g0 : g0 + PIECE],
+                MULT,
             )
 
-        def mult_v(n, s0, s1):
-            nc.vector.tensor_tensor(gy[n][:, s0:s1], y[n][:, s0:s1], gates[:, n, s0:s1], MULT)
+        for a in range(LAST):
+            if a == 0:
+                cast("vector", a, 0, 256)
+                cast("vector", a, 256, 512)
+                cast("scalar", a, 512, 768)
+            else:
+                split = VECTOR_FROM[a - 1]
+                cast("scalar", a, 0, PIECE)
+                if split > PIECE:
+                    cast("scalar", a, PIECE, split)
+                if split < T:
+                    cast("vector", a, split, T)
+            for t0 in range(0, T, PIECE):
+                quantize(a, t0, t0 + PIECE)
+            if PACKED and a == PACKED[-1]:
+                gather_bytes(PACKED[0], 0, T, WIDE)
+                for later in PACKED[1:]:
+                    shift(later)
+            for part in PARTS:
+                gather_words(a, part)
+            if a not in PACKED:
+                gather_bytes(a, 0, T, WIDE)
+        late_loads()
+        for t0 in range(0, T, PIECE):
+            cast("scalar", LAST, t0, t0 + PIECE)
+        quantize(LAST, 0, PIECE)
+        quantize(LAST, PIECE, EARLY)
+        for part in PARTS:
+            if part == PART_B:
+                quantize(LAST, EARLY, T)
+            gather_words(LAST, part)
+            gather_bytes(LAST, part[0], part[0] + PIECE, part[2])
 
-        def mult_g(n, s0, s1):
-            nc.gpsimd.tensor_tensor(gy[n][:, s0:s1], y[n][:, s0:s1], gates[:, n, s0:s1], MULT)
-
-        def scatter_copy(n, s0, s1):
-            nc.vector.tensor_copy(spread[n][:].indirect(offsets[:, s0 // 16 : s1 // 16]), gy[n][:, s0:s1])
-
-        def store(n):
-            nc.sync.dma_start(out=out[P * n : P * (n + 1), :], in_=spread[n][:, 0:T])
-
-        cast_v(0, 0, 384)
-        cast_s(0, 384, 512)
-        cast_s(0, 512, 768)
-        quantize(0, 0, 512)
-        quantize(0, 512, 768)
-        gather_words(0, 0, 768)
-        cast_v(1, 0, 256)
-        cast_s(1, 256, 512)
-        cast_s(1, 512, 768)
-        gather_bytes(0, 0, 768)
-        mm1(0)
-        mm0(0)
-        quantize(1, 0, 512)
-        quantize(1, 512, 768)
-        gather_words(1, 0, 768)
-        cast_v(2, 0, 128)
-        cast_s(2, 128, 512)
-        cast_s(2, 512, 768)
-        gather_bytes(1, 0, 768)
-        mm1(1)
-        mm0(1)
-        quantize(2, 0, 512)
-        quantize(2, 512, 768)
-        gather_words(2, 0, 768)
-        gather_bytes(2, 0, 768)
-        mm1(2)
-        mm0(2)
-        cast_s(3, 0, 256)
-        cast_s(3, 256, 512)
-        cast_s(3, 512, 768)
-        quantize(3, 0, 512)
-        quantize(3, 512, 768)
-        gather_words(3, 0, 256)
-        gather_bytes(3, 0, 256)
-        for n in range(N_BLOCKS):
-            mm0_last(n)
-            activate(0, n)
-        gather_words(3, 256, 768)
-        gather_bytes(3, 256, 768)
-        mm1(3)
-        for n in range(N_BLOCKS):
-            activate(1, n)
-        scatter(0, 0, 256)
-        scatter(1, 0, 256)
-        scatter(0, 256, 768)
-        store(0)
-        scatter(2, 0, 256)
-        scatter(1, 256, 768)
-        store(1)
-        scatter(2, 256, 768)
-        store(2)
+        for pair in range(0, len(groups), 2):
+            for a in range(PASSES):
+                multiply(a, pair)
+                multiply(a, pair + 1)
+            activate(pair)
+            activate(pair + 1)
+            n, part, h = groups[pair]
+            scatter(n, part)
+            if part == PART_C:
+                nc.sync.dma_start(out=out[P * n : P * (n + 1), :], in_=spread[n][:])

@@ -1,4 +1,5 @@
 import concourse.mybir as mybir
+from concourse.masks import make_identity
 
 K, T, E, N = 2048, 768, 2, 384
 FLOPS = 2 * T * K * N
@@ -14,7 +15,7 @@ PIECE = 256
 EARLY = 512
 WIDE = 1024
 PACKED = (0,1,2)
-VECTOR_FROM = (384, 384)
+VECTOR_SHARE = (448, 448)
 
 F32 = mybir.dt.float32
 BF16 = mybir.dt.bfloat16
@@ -53,6 +54,8 @@ def tile_moe_rag_lin_silu_kernel(tc, xT, w_words, w_scales, b, gate, offs, out):
         w_codes = [keep.tile([P, PASSES, 2 * N], U8, name="w_codes%d" % e, align_bytes=64) for e in range(E)]
         w_planes = keep.tile([P, E * PASSES, N], U8, name="w_planes", align_bytes=64)
         bias = keep.tile([P, N_BLOCKS, E], F32, name="bias")
+        bias_row = keep.tile([P, P * E], F32, name="bias_row")
+        identity = keep.tile([P, P], F32, name="identity")
         gates = [keep.tile([P, PIECE * (e + 1)], F32, name="gates%d" % e) for e in range(E)]
         probe = keep.tile([P, 1], F32, name="probe")
         y = [keep.tile([P, T], F32, name="y%d" % n) for n in range(N_BLOCKS)]
@@ -67,6 +70,7 @@ def tile_moe_rag_lin_silu_kernel(tc, xT, w_words, w_scales, b, gate, offs, out):
                 out=w_codes[e][:].bitcast(I32), in_=w_words[e].rearrange("a p c -> p a c").bitcast(I32)
             )
 
+        nc.gpsimd.memset(bias_row[:], 0.0)
         nc.vector.memset(probe[:], 0.0)
         nc.scalar.activation(probe[:], probe[:], SILU)
         planes = w_planes[:].rearrange("p g n -> p (g n)").bitcast(I32)
@@ -78,22 +82,27 @@ def tile_moe_rag_lin_silu_kernel(tc, xT, w_words, w_scales, b, gate, offs, out):
 
         nc.sync.dma_start(out=raw[0][:], in_=x_rows(0))
         nc.sync.dma_start(offsets[:], offs)
-        for a in range(1, LAST):
-            nc.sync.dma_start(out=raw[a][:], in_=x_rows(a))
+        nc.sync.dma_start(out=raw[1][:], in_=x_rows(1))
+        nc.sync.dma_start(out=bias_row[0:N_BLOCKS, :], in_=b.rearrange("(n p) e -> n (p e)", p=P))
+        nc.sync.dma_start(out=raw[2][:], in_=x_rows(2))
         nc.sync.dma_start(out=raw_early[:], in_=x_rows(LAST)[:, :, 0:EARLY])
-        nc.sync.dma_start(out=raw_late[:], in_=x_rows(LAST)[:, :, EARLY:T])
         for quadrant in range(4):
             nc.sync.dma_start(
                 out=planes[32 * quadrant : 32 * quadrant + 4, :].rearrange("r (g n) -> r g n", g=E * PASSES),
                 in_=w_scales[:, :, 4 * quadrant : 4 * quadrant + 4, :].rearrange("e a r n -> r (e a) n").bitcast(I32),
             )
+        nc.sync.dma_start(out=raw_late[:], in_=x_rows(LAST)[:, :, EARLY:T])
         load_w(1)
 
         def late_loads():
-            nc.sync.dma_start(out=bias[:], in_=b.rearrange("(c p) e -> p c e", p=P))
             nc.sync.dma_start(out=gates[1][:], in_=gate[0:P, PIECE:T])
             load_w(0)
             nc.sync.dma_start(out=gates[0][:], in_=gate[0:P, 0:PIECE])
+
+        make_identity(nc, identity[:])
+        for e in range(E):
+            nc.tensor.transpose(banks[7][:, P * e : P * (e + 1)], bias_row[:, e : E * P : E], identity[:])
+        nc.scalar.activation(bias[:], banks[7][:, 0 : E * P].rearrange("p (e n) -> p n e", e=E)[:, 0:N_BLOCKS, :], COPY)
 
         def cast(engine, a, t0, t1):
             if a < LAST:
@@ -183,19 +192,19 @@ def tile_moe_rag_lin_silu_kernel(tc, xT, w_words, w_scales, b, gate, offs, out):
                 cast("vector", a, 256, 512)
                 cast("scalar", a, 512, 768)
             else:
-                split = VECTOR_FROM[a - 1]
-                cast("scalar", a, 0, PIECE)
-                if split > PIECE:
-                    cast("scalar", a, PIECE, split)
-                if split < T:
-                    cast("vector", a, split, T)
+                split = PIECE + VECTOR_SHARE[a - 1]
+                cast("vector", a, 0, PIECE)
+                cast("scalar", a, PIECE, EARLY)
+                cast("vector", a, EARLY, split)
+                cast("scalar", a, split, T)
             for t0 in range(0, T, PIECE):
                 quantize(a, t0, t0 + PIECE)
+            gather_words(a, PART_A)
             if PACKED and a == PACKED[-1]:
                 gather_bytes(PACKED[0], 0, T, WIDE)
                 for later in PACKED[1:]:
                     shift(later)
-            for part in PARTS:
+            for part in PARTS[1:]:
                 gather_words(a, part)
             if a not in PACKED:
                 gather_bytes(a, 0, T, WIDE)

@@ -52,7 +52,7 @@ def tile_moe_rag_lin_silu_kernel(tc, xT, w_words, w_scales, b, gate, offs, out):
             slot_scales[a] = keep.tile([P, T], U8, name="slot_scales%d" % a, align_bytes=64)
         slot_words = [keep.tile([P, T], U32, name="slot_words%d" % a, align_bytes=64) for a in range(PASSES)]
         w_codes = [keep.tile([P, PASSES, 2 * N], U8, name="w_codes%d" % e, align_bytes=64) for e in range(E)]
-        w_planes = keep.tile([P, E * PASSES, N], U8, name="w_planes", align_bytes=64)
+        w_planes = [keep.tile([P, PASSES, N], U8, name="w_planes%d" % e, align_bytes=64) for e in range(E)]
         bias = keep.tile([P, N_BLOCKS, E], F32, name="bias")
         bias_row = keep.tile([P, P * E], F32, name="bias_row")
         identity = keep.tile([P, P], F32, name="identity")
@@ -71,10 +71,17 @@ def tile_moe_rag_lin_silu_kernel(tc, xT, w_words, w_scales, b, gate, offs, out):
             )
 
         nc.gpsimd.memset(bias_row[:], 0.0)
+        def load_scales(e):
+            for r in range(4):
+                nc.sync.dma_start(
+                    out=w_planes[e][r:P:32, :, :].bitcast(I32),
+                    in_=w_scales[e, :, r:16:4, :].rearrange("a q n -> q a n").bitcast(I32),
+                )
+
         nc.vector.memset(probe[:], 0.0)
         nc.scalar.activation(probe[:], probe[:], SILU)
-        planes = w_planes[:].rearrange("p g n -> p (g n)").bitcast(I32)
-        nc.vector.memset(planes, 0)
+        for e in range(E):
+            nc.vector.memset(w_planes[e][:].rearrange("p a n -> p (a n)").bitcast(I32), 0)
         for a in scales:
             nc.vector.memset(scales[a][:].bitcast(I32), 0)
         for a in PACKED[1:]:
@@ -86,16 +93,13 @@ def tile_moe_rag_lin_silu_kernel(tc, xT, w_words, w_scales, b, gate, offs, out):
         nc.sync.dma_start(out=bias_row[0:N_BLOCKS, :], in_=b.rearrange("(n p) e -> n (p e)", p=P))
         nc.sync.dma_start(out=raw[2][:], in_=x_rows(2))
         nc.sync.dma_start(out=raw_early[:], in_=x_rows(LAST)[:, :, 0:EARLY])
-        for quadrant in range(4):
-            nc.sync.dma_start(
-                out=planes[32 * quadrant : 32 * quadrant + 4, :].rearrange("r (g n) -> r g n", g=E * PASSES),
-                in_=w_scales[:, :, 4 * quadrant : 4 * quadrant + 4, :].rearrange("e a r n -> r (e a) n").bitcast(I32),
-            )
         nc.sync.dma_start(out=raw_late[:], in_=x_rows(LAST)[:, :, EARLY:T])
+        load_scales(1)
         load_w(1)
 
         def late_loads():
             nc.sync.dma_start(out=gates[1][:], in_=gate[0:P, PIECE:T])
+            load_scales(0)
             load_w(0)
             nc.sync.dma_start(out=gates[0][:], in_=gate[0:P, 0:PIECE])
 
@@ -163,7 +167,7 @@ def tile_moe_rag_lin_silu_kernel(tc, xT, w_words, w_scales, b, gate, offs, out):
             nc.tensor.matmul_mx(
                 out=acc(g),
                 lhsT=w_codes[e][:, a, 2 * P * n : 2 * P * (n + 1)].bitcast(E2M1X4),
-                lhsT_scale=w_planes[:, e * PASSES + a, P * n : P * (n + 1)],
+                lhsT_scale=w_planes[e][:, a, P * n : P * (n + 1)],
                 rhs=slot_words[a][:, s0 : s0 + P].bitcast(E4M3X4),
                 rhs_scale=slot_scales[a][:, s0 : s0 + P],
                 start=(a == 0),
@@ -209,8 +213,10 @@ def tile_moe_rag_lin_silu_kernel(tc, xT, w_words, w_scales, b, gate, offs, out):
             if a not in PACKED:
                 gather_bytes(a, 0, T, WIDE)
         late_loads()
-        for t0 in range(0, T, PIECE):
-            cast("scalar", LAST, t0, t0 + PIECE)
+        cast("scalar", LAST, 0, PIECE)
+        cast("scalar", LAST, PIECE, EARLY - 128)
+        cast("vector", LAST, EARLY - 128, EARLY)
+        cast("scalar", LAST, EARLY, T)
         quantize(LAST, 0, PIECE)
         quantize(LAST, PIECE, EARLY)
         for part in PARTS:

@@ -11,11 +11,16 @@ K_PASS = P * PACK
 PASSES = K // K_PASS
 LAST = PASSES - 1
 N_BLOCKS = N // P
+BANKS = 8
 PIECE = 256
-EARLY = 512
 WIDE = 1024
-PACKED = (0,1,2)
-VECTOR_SHARE = (448, 448)
+PLANE_STEP = 4
+SHIFT_ROWS = 112
+RUN = 4
+
+VECTOR_SHARE = (512, 448, 448, 352)
+
+PARTS = ((256, 1, 2 * PIECE), (512, 1, T), (0, 0, T))
 
 F32 = mybir.dt.float32
 BF16 = mybir.dt.bfloat16
@@ -29,159 +34,122 @@ COPY = mybir.ActivationFunctionType.Copy
 SILU = mybir.ActivationFunctionType.Silu
 MULT = mybir.AluOpType.mult
 
-PART_A = (256, 1, EARLY)
-PART_B = (512, 1, T)
-PART_C = (0, 0, T)
-PARTS = (PART_A, PART_B, PART_C)
-
 
 def tile_moe_rag_lin_silu_kernel(tc, xT, w_words, w_scales, b, gate, offs, out):
     nc = tc.nc
     with tc.tile_pool(name="keep", bufs=1) as keep, tc.psum_pool(name="psum", bufs=1) as psum:
         offsets = keep.tile([P, T // 16], U16, name="offsets")
-        raw = [keep.tile([P, PACK, T], F32, name="raw%d" % a, align_bytes=64) for a in range(LAST)]
-        raw_early = keep.tile([P, PACK, EARLY], F32, name="raw_early", align_bytes=64)
-        raw_late = keep.tile([P, PACK, T - EARLY], F32, name="raw_late", align_bytes=64)
+        raw = [keep.tile([P, PACK, T], F32, name="raw%d" % a, align_bytes=64) for a in range(PASSES)]
         grouped = [keep.tile([P, T, PACK], BF16, name="grouped%d" % a, align_bytes=64) for a in range(PASSES)]
         words = [keep.tile([P, T], I32, name="words%d" % a, align_bytes=64) for a in range(PASSES)]
-        scales = {}
-        slot_scales = {}
-        for a in range(PASSES):
-            if a not in PACKED[1:]:
-                scales[a] = keep.tile([P, WIDE], U8, name="scales%d" % a, align_bytes=64)
-            slot_scales[a] = keep.tile([P, T], U8, name="slot_scales%d" % a, align_bytes=64)
+        shared_planes = keep.tile([P, WIDE], U8, name="shared_planes", align_bytes=64)
+        last_plane = keep.tile([P, WIDE], U8, name="last_plane", align_bytes=64)
         slot_words = [keep.tile([P, T], U32, name="slot_words%d" % a, align_bytes=64) for a in range(PASSES)]
+        slot_planes = [keep.tile([P, T], U8, name="slot_planes%d" % a, align_bytes=64) for a in range(PASSES)]
         w_codes = [keep.tile([P, PASSES, 2 * N], U8, name="w_codes%d" % e, align_bytes=64) for e in range(E)]
         w_planes = [keep.tile([P, PASSES, N], U8, name="w_planes%d" % e, align_bytes=64) for e in range(E)]
-        bias = keep.tile([P, N_BLOCKS, E], F32, name="bias")
-        bias_row = keep.tile([P, P * E], F32, name="bias_row")
+        bias_rows = keep.tile([P, P * E], F32, name="bias_rows")
         identity = keep.tile([P, P], F32, name="identity")
+        bias = keep.tile([P, N_BLOCKS, E], F32, name="bias")
         gates = [keep.tile([P, PIECE * (e + 1)], F32, name="gates%d" % e) for e in range(E)]
-        probe = keep.tile([P, 1], F32, name="probe")
+        warm_up = keep.tile([P, 1], F32, name="warm_up")
         y = [keep.tile([P, T], F32, name="y%d" % n) for n in range(N_BLOCKS)]
         spread = [keep.tile([P, T], F32, name="spread%d" % n) for n in range(N_BLOCKS)]
-        banks = [psum.tile([P, 512], F32, name="bank%d" % i) for i in range(8)]
+        banks = [psum.tile([P, 512], F32, name="bank%d" % i) for i in range(BANKS)]
 
-        def x_rows(a):
-            return xT[a * K_PASS : (a + 1) * K_PASS, :].rearrange("(p j) w -> p j w", j=PACK)
+        def load_x(a):
+            rows = xT[a * K_PASS : (a + 1) * K_PASS, :].rearrange("(p j) t -> p j t", j=PACK)
+            nc.sync.dma_start(out=raw[a][:], in_=rows)
 
-        def load_w(e):
-            nc.sync.dma_start(
-                out=w_codes[e][:].bitcast(I32), in_=w_words[e].rearrange("a p c -> p a c").bitcast(I32)
-            )
-
-        nc.gpsimd.memset(bias_row[:], 0.0)
-        def load_scales(e):
+        def load_expert(e):
             for r in range(4):
                 nc.sync.dma_start(
                     out=w_planes[e][r:P:32, :, :].bitcast(I32),
                     in_=w_scales[e, :, r:16:4, :].rearrange("a q n -> q a n").bitcast(I32),
                 )
+            nc.sync.dma_start(
+                out=w_codes[e][:].bitcast(I32), in_=w_words[e].rearrange("a p c -> p a c").bitcast(I32)
+            )
 
-        nc.vector.memset(probe[:], 0.0)
-        nc.scalar.activation(probe[:], probe[:], SILU)
-        for e in range(E):
-            nc.vector.memset(w_planes[e][:].rearrange("p a n -> p (a n)").bitcast(I32), 0)
-        for a in scales:
-            nc.vector.memset(scales[a][:].bitcast(I32), 0)
-        for a in PACKED[1:]:
-            nc.vector.memset(slot_scales[a][:].bitcast(I32), 0)
+        def load_gate(e):
+            nc.sync.dma_start(out=gates[e][:], in_=gate[0:P, PIECE * e : PIECE * (2 * e + 1)])
 
-        nc.sync.dma_start(out=raw[0][:], in_=x_rows(0))
-        nc.sync.dma_start(offsets[:], offs)
-        nc.sync.dma_start(out=raw[1][:], in_=x_rows(1))
-        nc.sync.dma_start(out=bias_row[0:N_BLOCKS, :], in_=b.rearrange("(n p) e -> n (p e)", p=P))
-        nc.sync.dma_start(out=raw[2][:], in_=x_rows(2))
-        nc.sync.dma_start(out=raw_early[:], in_=x_rows(LAST)[:, :, 0:EARLY])
-        nc.sync.dma_start(out=raw_late[:], in_=x_rows(LAST)[:, :, EARLY:T])
-        load_scales(1)
-        load_w(1)
-
-        def late_loads():
-            nc.sync.dma_start(out=gates[1][:], in_=gate[0:P, PIECE:T])
-            load_scales(0)
-            load_w(0)
-            nc.sync.dma_start(out=gates[0][:], in_=gate[0:P, 0:PIECE])
-
-        make_identity(nc, identity[:])
-        for e in range(E):
-            nc.tensor.transpose(banks[7][:, P * e : P * (e + 1)], bias_row[:, e : E * P : E], identity[:])
-        nc.scalar.activation(bias[:], banks[7][:, 0 : E * P].rearrange("p (e n) -> p n e", e=E)[:, 0:N_BLOCKS, :], COPY)
-
-        def cast(engine, a, t0, t1):
-            if a < LAST:
-                src = raw[a][:, :, t0:t1]
-            elif t0 < EARLY:
-                src = raw_early[:, :, t0:t1]
-            else:
-                src = raw_late[:, :, t0 - EARLY : t1 - EARLY]
-            dst = grouped[a][:, t0:t1, :].rearrange("p (c i) j -> p c j i", i=4)
-            src = src.rearrange("p j (c i) -> p c j i", i=4)
-            if engine == "vector":
+        def round_tokens(on_vector, a, t0, t1):
+            dst = grouped[a][:, t0:t1, :].rearrange("p (c i) j -> p c j i", i=RUN)
+            src = raw[a][:, :, t0:t1].rearrange("p j (c i) -> p c j i", i=RUN)
+            if on_vector:
                 nc.vector.tensor_copy(dst, src)
             else:
                 nc.scalar.activation(dst, src, COPY)
 
-        def quantize(a, t0, t1):
-            if a in PACKED:
-                plane = scales[PACKED[0]][4 * PACKED.index(a) : P, t0:t1]
+        def round_pass(a):
+            if a == 0:
+                round_tokens(True, a, 0, PIECE)
+                round_tokens(True, a, PIECE, VECTOR_SHARE[a])
+                round_tokens(False, a, VECTOR_SHARE[a], T)
             else:
-                plane = scales[a][:, t0:t1]
+                cut = PIECE + VECTOR_SHARE[a]
+                round_tokens(True, a, 0, PIECE)
+                round_tokens(False, a, PIECE, 2 * PIECE)
+                round_tokens(True, a, 2 * PIECE, cut)
+                round_tokens(False, a, cut, T)
+
+        def quantize(a, t0):
+            plane = last_plane if a == LAST else shared_planes
+            first_row = 0 if a == LAST else PLANE_STEP * a
             nc.vector.quantize_mx(
-                out=words[a][:, t0:t1].bitcast(E4M3X4),
-                scales=plane,
-                in_=grouped[a][:, t0:t1, :].rearrange("p t j -> p (t j)"),
+                out=words[a][:, t0 : t0 + PIECE].bitcast(E4M3X4),
+                scales=plane[first_row:P, t0 : t0 + PIECE],
+                in_=grouped[a][:, t0 : t0 + PIECE, :].rearrange("p t j -> p (t j)"),
             )
 
         def entries(s0, s1):
             return offsets[:, s0 // 16 : s1 // 16]
 
         def gather_words(a, part):
-            s0, e, width = part
-            nc.vector.tensor_copy(
-                slot_words[a][:, s0 : s0 + PIECE], words[a][:, 0:width].bitcast(U32).indirect(entries(s0, s0 + PIECE))
-            )
+            s0, e, columns = part
+            window = words[a][:, 0:columns].bitcast(U32)
+            nc.vector.tensor_copy(slot_words[a][:, s0 : s0 + PIECE], window.indirect(entries(s0, s0 + PIECE)))
 
-        def gather_bytes(a, s0, s1, width):
-            nc.vector.tensor_copy(slot_scales[a][:, s0:s1], scales[a][:, 0:width].indirect(entries(s0, s1)))
+        def gather_last_plane(part):
+            s0, e, columns = part
+            window = last_plane[:, 0:columns]
+            nc.vector.tensor_copy(slot_planes[LAST][:, s0 : s0 + PIECE], window.indirect(entries(s0, s0 + PIECE)))
 
-        def shift(a):
-            first = 4 * PACKED.index(a)
-            nc.sync.dma_start(
-                out=slot_scales[a][0:112, :].bitcast(I32),
-                in_=slot_scales[PACKED[0]][first : first + 112, :].bitcast(I32),
-            )
+        def gather_shared_planes():
+            nc.vector.tensor_copy(slot_planes[0][:], shared_planes[:].indirect(entries(0, T)))
+            for a in range(1, LAST):
+                nc.sync.dma_start(
+                    out=slot_planes[a][0:SHIFT_ROWS, :].bitcast(I32),
+                    in_=slot_planes[0][PLANE_STEP * a : PLANE_STEP * a + SHIFT_ROWS, :].bitcast(I32),
+                )
 
-        groups = [(n, PART_A, h) for n in range(N_BLOCKS) for h in range(2)]
-        groups = groups + [(n, part, h) for n in range(N_BLOCKS) for part in (PART_B, PART_C) for h in range(2)]
+        groups = [(n, part, half) for part in PARTS for n in range(N_BLOCKS) for half in range(PIECE // P)]
 
-        def acc(g):
-            late = g - 6
-            bank, turn = (g, 0) if g < 8 else ((late - 2) % 8, 1 + (late - 2) // 8)
+        def accumulator(g):
+            turn, bank = divmod(g, BANKS)
             return banks[bank][:, P * turn : P * (turn + 1)]
 
         def multiply(a, g):
-            n, part, h = groups[g]
-            s0 = part[0] + P * h
-            e = part[1]
+            n, (s0, e, columns), half = groups[g]
+            slots = slice(s0 + P * half, s0 + P * (half + 1))
             nc.tensor.matmul_mx(
-                out=acc(g),
+                out=accumulator(g),
                 lhsT=w_codes[e][:, a, 2 * P * n : 2 * P * (n + 1)].bitcast(E2M1X4),
                 lhsT_scale=w_planes[e][:, a, P * n : P * (n + 1)],
-                rhs=slot_words[a][:, s0 : s0 + P].bitcast(E4M3X4),
-                rhs_scale=slot_scales[a][:, s0 : s0 + P],
+                rhs=slot_words[a][:, slots].bitcast(E4M3X4),
+                rhs_scale=slot_planes[a][:, slots],
                 start=(a == 0),
                 stop=(a == LAST),
             )
 
         def activate(g):
-            n, part, h = groups[g]
-            s0 = part[0] + P * h
-            e = part[1]
-            nc.scalar.activation(y[n][:, s0 : s0 + P], acc(g), SILU, bias=bias[:, n, e : e + 1])
+            n, (s0, e, columns), half = groups[g]
+            slots = slice(s0 + P * half, s0 + P * (half + 1))
+            nc.scalar.activation(y[n][:, slots], accumulator(g), SILU, bias=bias[:, n, e : e + 1])
 
         def scatter(n, part):
-            s0, e, width = part
+            s0, e, columns = part
             g0 = s0 - PIECE * e
             nc.vector.tensor_tensor(
                 spread[n][:].indirect(entries(s0, s0 + PIECE)),
@@ -190,48 +158,58 @@ def tile_moe_rag_lin_silu_kernel(tc, xT, w_words, w_scales, b, gate, offs, out):
                 MULT,
             )
 
+        nc.gpsimd.memset(bias_rows[:], 0.0)
+        nc.vector.memset(warm_up[:], 0.0)
+        nc.scalar.activation(warm_up[:], warm_up[:], SILU)
+        for e in range(E):
+            nc.vector.memset(w_planes[e][:].rearrange("p a n -> p (a n)").bitcast(I32), 0)
+        nc.vector.memset(shared_planes[:].bitcast(I32), 0)
+        nc.vector.memset(last_plane[:].bitcast(I32), 0)
+        for a in range(1, LAST):
+            nc.vector.memset(slot_planes[a][:].bitcast(I32), 0)
+
+        load_x(0)
+        nc.sync.dma_start(offsets[:], offs)
+        load_x(1)
+        nc.sync.dma_start(out=bias_rows[0:N_BLOCKS, :], in_=b.rearrange("(n p) e -> n (p e)", p=P))
+        for a in range(2, PASSES):
+            load_x(a)
+        load_expert(1)
+
+        make_identity(nc, identity[:])
+        turned = banks[BANKS - 1]
+        for e in range(E):
+            nc.tensor.transpose(turned[:, P * e : P * (e + 1)], bias_rows[:, e : E * P : E], identity[:])
+        nc.scalar.activation(bias[:], turned[:, 0 : E * P].rearrange("p (e n) -> p n e", e=E)[:, 0:N_BLOCKS, :], COPY)
+
         for a in range(LAST):
-            if a == 0:
-                cast("vector", a, 0, 256)
-                cast("vector", a, 256, 512)
-                cast("scalar", a, 512, 768)
-            else:
-                split = PIECE + VECTOR_SHARE[a - 1]
-                cast("vector", a, 0, PIECE)
-                cast("scalar", a, PIECE, EARLY)
-                cast("vector", a, EARLY, split)
-                cast("scalar", a, split, T)
+            round_pass(a)
             for t0 in range(0, T, PIECE):
-                quantize(a, t0, t0 + PIECE)
-            gather_words(a, PART_A)
-            if PACKED and a == PACKED[-1]:
-                gather_bytes(PACKED[0], 0, T, WIDE)
-                for later in PACKED[1:]:
-                    shift(later)
+                quantize(a, t0)
+            gather_words(a, PARTS[0])
+            if a == LAST - 1:
+                gather_shared_planes()
             for part in PARTS[1:]:
                 gather_words(a, part)
-            if a not in PACKED:
-                gather_bytes(a, 0, T, WIDE)
-        late_loads()
-        cast("scalar", LAST, 0, PIECE)
-        cast("scalar", LAST, PIECE, EARLY - 128)
-        cast("vector", LAST, EARLY - 128, EARLY)
-        cast("scalar", LAST, EARLY, T)
-        quantize(LAST, 0, PIECE)
-        quantize(LAST, PIECE, EARLY)
-        for part in PARTS:
-            if part == PART_B:
-                quantize(LAST, EARLY, T)
-            gather_words(LAST, part)
-            gather_bytes(LAST, part[0], part[0] + PIECE, part[2])
 
-        for pair in range(0, len(groups), 2):
+        load_gate(1)
+        load_expert(0)
+        load_gate(0)
+
+        round_pass(LAST)
+        for t0 in range(0, T, PIECE):
+            quantize(LAST, t0)
+        for part in PARTS:
+            gather_words(LAST, part)
+            gather_last_plane(part)
+
+        for g in range(0, len(groups), 2):
             for a in range(PASSES):
-                multiply(a, pair)
-                multiply(a, pair + 1)
-            activate(pair)
-            activate(pair + 1)
-            n, part, h = groups[pair]
+                multiply(a, g)
+                multiply(a, g + 1)
+            activate(g)
+            activate(g + 1)
+            n, part, half = groups[g]
             scatter(n, part)
-            if part == PART_C:
+            if part == PARTS[-1]:
                 nc.sync.dma_start(out=out[P * n : P * (n + 1), :], in_=spread[n][:])

@@ -20,7 +20,9 @@ RUN = 4
 
 VECTOR_SHARE = (512, 448, 448, 352)
 
-PARTS = ((256, 1, 2 * PIECE), (512, 1, T), (0, 0, T))
+EARLY, SPARSE, LATE = (256, 1, 2 * PIECE), (0, 0, T), (512, 1, T)
+PARTS = (EARLY, SPARSE, LATE)
+
 
 F32 = mybir.dt.float32
 BF16 = mybir.dt.bfloat16
@@ -47,11 +49,12 @@ def tile_moe_rag_lin_silu_kernel(tc, xT, w_words, w_scales, b, gate, offs, out):
         slot_words = [keep.tile([P, T], U32, name="slot_words%d" % a, align_bytes=64) for a in range(PASSES)]
         slot_planes = [keep.tile([P, T], U8, name="slot_planes%d" % a, align_bytes=64) for a in range(PASSES)]
         w_codes = [keep.tile([P, PASSES, 2 * N], U8, name="w_codes%d" % e, align_bytes=64) for e in range(E)]
-        w_planes = [keep.tile([P, PASSES, N], U8, name="w_planes%d" % e, align_bytes=64) for e in range(E)]
+        w_planes = keep.tile([P, E * PASSES, N], U8, name="w_planes", align_bytes=64)
         bias_rows = keep.tile([P, P * E], F32, name="bias_rows")
         identity = keep.tile([P, P], F32, name="identity")
         bias = keep.tile([P, N_BLOCKS, E], F32, name="bias")
-        gates = [keep.tile([P, PIECE * (e + 1)], F32, name="gates%d" % e) for e in range(E)]
+        gates = keep.tile([P, T], F32, name="gates")
+        gated = [keep.tile([P, PIECE], F32, name="gated%d" % n) for n in range(N_BLOCKS)]
         warm_up = keep.tile([P, 1], F32, name="warm_up")
         y = [keep.tile([P, T], F32, name="y%d" % n) for n in range(N_BLOCKS)]
         spread = [keep.tile([P, T], F32, name="spread%d" % n) for n in range(N_BLOCKS)]
@@ -61,18 +64,17 @@ def tile_moe_rag_lin_silu_kernel(tc, xT, w_words, w_scales, b, gate, offs, out):
             rows = xT[a * K_PASS : (a + 1) * K_PASS, :].rearrange("(p j) t -> p j t", j=PACK)
             nc.sync.dma_start(out=raw[a][:], in_=rows)
 
-        def load_expert(e):
+        def load_scales():
             for r in range(4):
                 nc.sync.dma_start(
-                    out=w_planes[e][r:P:32, :, :].bitcast(I32),
-                    in_=w_scales[e, :, r:16:4, :].rearrange("a q n -> q a n").bitcast(I32),
+                    out=w_planes[r:P:32, :, :].bitcast(I32),
+                    in_=w_scales[:, :, r:16:4, :].rearrange("e a q n -> q (e a) n").bitcast(I32),
                 )
+
+        def load_codes(e):
             nc.sync.dma_start(
                 out=w_codes[e][:].bitcast(I32), in_=w_words[e].rearrange("a p c -> p a c").bitcast(I32)
             )
-
-        def load_gate(e):
-            nc.sync.dma_start(out=gates[e][:], in_=gate[0:P, PIECE * e : PIECE * (2 * e + 1)])
 
         def round_tokens(on_vector, a, t0, t1):
             dst = grouped[a][:, t0:t1, :].rearrange("p (c i) j -> p c j i", i=RUN)
@@ -124,19 +126,19 @@ def tile_moe_rag_lin_silu_kernel(tc, xT, w_words, w_scales, b, gate, offs, out):
                     in_=slot_planes[0][PLANE_STEP * a : PLANE_STEP * a + SHIFT_ROWS, :].bitcast(I32),
                 )
 
-        groups = [(n, part, half) for part in PARTS for n in range(N_BLOCKS) for half in range(PIECE // P)]
+        groups = [(n, part) for n in range(N_BLOCKS) for part in (EARLY, SPARSE)] + [(n, LATE) for n in range(N_BLOCKS)]
 
         def accumulator(g):
             turn, bank = divmod(g, BANKS)
-            return banks[bank][:, P * turn : P * (turn + 1)]
+            return banks[bank][:, PIECE * turn : PIECE * (turn + 1)]
 
         def multiply(a, g):
-            n, (s0, e, columns), half = groups[g]
-            slots = slice(s0 + P * half, s0 + P * (half + 1))
+            n, (s0, e, columns) = groups[g]
+            slots = slice(s0, s0 + PIECE)
             nc.tensor.matmul_mx(
                 out=accumulator(g),
                 lhsT=w_codes[e][:, a, 2 * P * n : 2 * P * (n + 1)].bitcast(E2M1X4),
-                lhsT_scale=w_planes[e][:, a, P * n : P * (n + 1)],
+                lhsT_scale=w_planes[:, PASSES * e + a, P * n : P * (n + 1)],
                 rhs=slot_words[a][:, slots].bitcast(E4M3X4),
                 rhs_scale=slot_planes[a][:, slots],
                 start=(a == 0),
@@ -144,25 +146,22 @@ def tile_moe_rag_lin_silu_kernel(tc, xT, w_words, w_scales, b, gate, offs, out):
             )
 
         def activate(g):
-            n, (s0, e, columns), half = groups[g]
-            slots = slice(s0 + P * half, s0 + P * (half + 1))
-            nc.scalar.activation(y[n][:, slots], accumulator(g), SILU, bias=bias[:, n, e : e + 1])
+            n, (s0, e, columns) = groups[g]
+            nc.scalar.activation(y[n][:, s0 : s0 + PIECE], accumulator(g), SILU, bias=bias[:, n, e : e + 1])
 
         def scatter(n, part):
-            s0, e, columns = part
-            g0 = s0 - PIECE * e
-            nc.vector.tensor_tensor(
-                spread[n][:].indirect(entries(s0, s0 + PIECE)),
-                y[n][:, s0 : s0 + PIECE],
-                gates[e][:, g0 : g0 + PIECE],
-                MULT,
-            )
+            slots = slice(part[0], part[0] + PIECE)
+            window = spread[n][:].indirect(entries(slots.start, slots.stop))
+            if part == SPARSE:
+                nc.vector.tensor_tensor(gated[n][:], y[n][:, slots], gates[:, slots], MULT)
+                nc.scalar.activation(window, gated[n][:], COPY)
+            else:
+                nc.vector.tensor_tensor(window, y[n][:, slots], gates[:, slots], MULT)
 
         nc.gpsimd.memset(bias_rows[:], 0.0)
         nc.vector.memset(warm_up[:], 0.0)
         nc.scalar.activation(warm_up[:], warm_up[:], SILU)
-        for e in range(E):
-            nc.vector.memset(w_planes[e][:].rearrange("p a n -> p (a n)").bitcast(I32), 0)
+        nc.vector.memset(w_planes[:].rearrange("p a n -> p (a n)").bitcast(I32), 0)
         nc.vector.memset(shared_planes[:].bitcast(I32), 0)
         nc.vector.memset(last_plane[:].bitcast(I32), 0)
         for a in range(1, LAST):
@@ -174,7 +173,9 @@ def tile_moe_rag_lin_silu_kernel(tc, xT, w_words, w_scales, b, gate, offs, out):
         nc.sync.dma_start(out=bias_rows[0:N_BLOCKS, :], in_=b.rearrange("(n p) e -> n (p e)", p=P))
         for a in range(2, PASSES):
             load_x(a)
-        load_expert(1)
+        load_scales()
+        load_codes(1)
+        load_codes(0)
 
         make_identity(nc, identity[:])
         turned = banks[BANKS - 1]
@@ -192,9 +193,7 @@ def tile_moe_rag_lin_silu_kernel(tc, xT, w_words, w_scales, b, gate, offs, out):
             for part in PARTS[1:]:
                 gather_words(a, part)
 
-        load_gate(1)
-        load_expert(0)
-        load_gate(0)
+        nc.sync.dma_start(out=gates[:], in_=gate[0:P, :])
 
         round_pass(LAST)
         for t0 in range(0, T, PIECE):
@@ -203,13 +202,14 @@ def tile_moe_rag_lin_silu_kernel(tc, xT, w_words, w_scales, b, gate, offs, out):
             gather_words(LAST, part)
             gather_last_plane(part)
 
-        for g in range(0, len(groups), 2):
+        for g in range(len(groups)):
             for a in range(PASSES):
                 multiply(a, g)
-                multiply(a, g + 1)
             activate(g)
-            activate(g + 1)
-            n, part, half = groups[g]
-            scatter(n, part)
-            if part == PARTS[-1]:
-                nc.sync.dma_start(out=out[P * n : P * (n + 1), :], in_=spread[n][:])
+
+        for n in range(N_BLOCKS):
+            scatter(n, EARLY)
+            scatter(n, SPARSE)
+        for n in range(N_BLOCKS):
+            scatter(n, LATE)
+            nc.sync.dma_start(out=out[P * n : P * (n + 1), :], in_=spread[n][:])

@@ -18,10 +18,11 @@ PLANE_STEP = 4
 SHIFT_ROWS = 112
 RUN = 4
 
-VECTOR_SHARE = (512, 448, 448, 352)
+VECTOR_SHARE = (512, 448, 448, 448)
 
 EARLY, SPARSE, LATE = (256, 1, 2 * PIECE), (0, 0, T), (512, 1, T)
 PARTS = (EARLY, SPARSE, LATE)
+SCALAR_BLOCKS = 3
 
 
 F32 = mybir.dt.float32
@@ -49,12 +50,12 @@ def tile_moe_rag_lin_silu_kernel(tc, xT, w_words, w_scales, b, gate, offs, out):
         slot_words = [keep.tile([P, T], U32, name="slot_words%d" % a, align_bytes=64) for a in range(PASSES)]
         slot_planes = [keep.tile([P, T], U8, name="slot_planes%d" % a, align_bytes=64) for a in range(PASSES)]
         w_codes = [keep.tile([P, PASSES, 2 * N], U8, name="w_codes%d" % e, align_bytes=64) for e in range(E)]
-        w_planes = keep.tile([P, E * PASSES, N], U8, name="w_planes", align_bytes=64)
+        w_planes = [keep.tile([P, PASSES, N], U8, name="w_planes%d" % e, align_bytes=64) for e in range(E)]
         bias_rows = keep.tile([P, P * E], F32, name="bias_rows")
         identity = keep.tile([P, P], F32, name="identity")
         bias = keep.tile([P, N_BLOCKS, E], F32, name="bias")
-        gates = keep.tile([P, T], F32, name="gates")
-        gated = [keep.tile([P, PIECE], F32, name="gated%d" % n) for n in range(N_BLOCKS)]
+        gates = [keep.tile([P, PIECE * (e + 1)], F32, name="gates%d" % e) for e in range(E)]
+        gated = [keep.tile([P, PIECE], F32, name="gated%d" % n) for n in range(SCALAR_BLOCKS)]
         warm_up = keep.tile([P, 1], F32, name="warm_up")
         y = [keep.tile([P, T], F32, name="y%d" % n) for n in range(N_BLOCKS)]
         spread = [keep.tile([P, T], F32, name="spread%d" % n) for n in range(N_BLOCKS)]
@@ -64,17 +65,20 @@ def tile_moe_rag_lin_silu_kernel(tc, xT, w_words, w_scales, b, gate, offs, out):
             rows = xT[a * K_PASS : (a + 1) * K_PASS, :].rearrange("(p j) t -> p j t", j=PACK)
             nc.sync.dma_start(out=raw[a][:], in_=rows)
 
-        def load_scales():
+        def load_scales(e):
             for r in range(4):
                 nc.sync.dma_start(
-                    out=w_planes[r:P:32, :, :].bitcast(I32),
-                    in_=w_scales[:, :, r:16:4, :].rearrange("e a q n -> q (e a) n").bitcast(I32),
+                    out=w_planes[e][r:P:32, :, :].bitcast(I32),
+                    in_=w_scales[e, :, r:16:4, :].rearrange("a q n -> q a n").bitcast(I32),
                 )
 
         def load_codes(e):
             nc.sync.dma_start(
                 out=w_codes[e][:].bitcast(I32), in_=w_words[e].rearrange("a p c -> p a c").bitcast(I32)
             )
+
+        def load_gate(e):
+            nc.sync.dma_start(out=gates[e][:], in_=gate[0:P, PIECE * e : PIECE * (2 * e + 1)])
 
         def round_tokens(on_vector, a, t0, t1):
             dst = grouped[a][:, t0:t1, :].rearrange("p (c i) j -> p c j i", i=RUN)
@@ -138,7 +142,7 @@ def tile_moe_rag_lin_silu_kernel(tc, xT, w_words, w_scales, b, gate, offs, out):
             nc.tensor.matmul_mx(
                 out=accumulator(g),
                 lhsT=w_codes[e][:, a, 2 * P * n : 2 * P * (n + 1)].bitcast(E2M1X4),
-                lhsT_scale=w_planes[:, PASSES * e + a, P * n : P * (n + 1)],
+                lhsT_scale=w_planes[e][:, a, P * n : P * (n + 1)],
                 rhs=slot_words[a][:, slots].bitcast(E4M3X4),
                 rhs_scale=slot_planes[a][:, slots],
                 start=(a == 0),
@@ -150,18 +154,25 @@ def tile_moe_rag_lin_silu_kernel(tc, xT, w_words, w_scales, b, gate, offs, out):
             nc.scalar.activation(y[n][:, s0 : s0 + PIECE], accumulator(g), SILU, bias=bias[:, n, e : e + 1])
 
         def scatter(n, part):
-            slots = slice(part[0], part[0] + PIECE)
-            window = spread[n][:].indirect(entries(slots.start, slots.stop))
-            if part == SPARSE:
-                nc.vector.tensor_tensor(gated[n][:], y[n][:, slots], gates[:, slots], MULT)
-                nc.scalar.activation(window, gated[n][:], COPY)
-            else:
-                nc.vector.tensor_tensor(window, y[n][:, slots], gates[:, slots], MULT)
+            s0, e, columns = part
+            g0 = s0 - PIECE * e
+            window = spread[n][:].indirect(entries(s0, s0 + PIECE))
+            nc.vector.tensor_tensor(window, y[n][:, s0 : s0 + PIECE], gates[e][:, g0 : g0 + PIECE], MULT)
+
+        def apply_gate(n):
+            nc.vector.tensor_tensor(gated[n][:], y[n][:, 0:PIECE], gates[0][:], MULT)
+
+        def scatter_gated(n):
+            nc.scalar.activation(spread[n][:].indirect(entries(0, PIECE)), gated[n][:], COPY)
+
+        def store(n):
+            nc.sync.dma_start(out=out[P * n : P * (n + 1), :], in_=spread[n][:])
 
         nc.gpsimd.memset(bias_rows[:], 0.0)
         nc.vector.memset(warm_up[:], 0.0)
         nc.scalar.activation(warm_up[:], warm_up[:], SILU)
-        nc.vector.memset(w_planes[:].rearrange("p a n -> p (a n)").bitcast(I32), 0)
+        for e in range(E):
+            nc.vector.memset(w_planes[e][:].rearrange("p a n -> p (a n)").bitcast(I32), 0)
         nc.vector.memset(shared_planes[:].bitcast(I32), 0)
         nc.vector.memset(last_plane[:].bitcast(I32), 0)
         for a in range(1, LAST):
@@ -171,11 +182,11 @@ def tile_moe_rag_lin_silu_kernel(tc, xT, w_words, w_scales, b, gate, offs, out):
         nc.sync.dma_start(offsets[:], offs)
         load_x(1)
         nc.sync.dma_start(out=bias_rows[0:N_BLOCKS, :], in_=b.rearrange("(n p) e -> n (p e)", p=P))
-        for a in range(2, PASSES):
-            load_x(a)
-        load_scales()
+        load_x(2)
+        load_scales(1)
         load_codes(1)
-        load_codes(0)
+        load_x(3)
+        load_scales(0)
 
         make_identity(nc, identity[:])
         turned = banks[BANKS - 1]
@@ -193,7 +204,9 @@ def tile_moe_rag_lin_silu_kernel(tc, xT, w_words, w_scales, b, gate, offs, out):
             for part in PARTS[1:]:
                 gather_words(a, part)
 
-        nc.sync.dma_start(out=gates[:], in_=gate[0:P, :])
+        load_codes(0)
+        load_gate(0)
+        load_gate(1)
 
         round_pass(LAST)
         for t0 in range(0, T, PIECE):
@@ -209,7 +222,8 @@ def tile_moe_rag_lin_silu_kernel(tc, xT, w_words, w_scales, b, gate, offs, out):
 
         for n in range(N_BLOCKS):
             scatter(n, EARLY)
-            scatter(n, SPARSE)
+            apply_gate(n)
+            scatter_gated(n)
         for n in range(N_BLOCKS):
             scatter(n, LATE)
-            nc.sync.dma_start(out=out[P * n : P * (n + 1), :], in_=spread[n][:])
+            store(n)

@@ -22,7 +22,6 @@ VECTOR_SHARE = (512, 448, 448, 448)
 
 EARLY, SPARSE, LATE = (256, 1, 2 * PIECE), (0, 0, T), (512, 1, T)
 PARTS = (EARLY, SPARSE, LATE)
-SCALAR_BLOCKS = 3
 
 
 F32 = mybir.dt.float32
@@ -55,7 +54,7 @@ def tile_moe_rag_lin_silu_kernel(tc, xT, w_words, w_scales, b, gate, offs, out):
         identity = keep.tile([P, P], F32, name="identity")
         bias = keep.tile([P, N_BLOCKS, E], F32, name="bias")
         gates = [keep.tile([P, PIECE * (e + 1)], F32, name="gates%d" % e) for e in range(E)]
-        gated = [keep.tile([P, PIECE], F32, name="gated%d" % n) for n in range(SCALAR_BLOCKS)]
+        gated = keep.tile([P, PIECE], F32, name="gated")
         warm_up = keep.tile([P, 1], F32, name="warm_up")
         y = [keep.tile([P, T], F32, name="y%d" % n) for n in range(N_BLOCKS)]
         spread = [keep.tile([P, T], F32, name="spread%d" % n) for n in range(N_BLOCKS)]
@@ -130,7 +129,7 @@ def tile_moe_rag_lin_silu_kernel(tc, xT, w_words, w_scales, b, gate, offs, out):
                     in_=slot_planes[0][PLANE_STEP * a : PLANE_STEP * a + SHIFT_ROWS, :].bitcast(I32),
                 )
 
-        groups = [(n, part) for n in range(N_BLOCKS) for part in (EARLY, SPARSE)] + [(n, LATE) for n in range(N_BLOCKS)]
+        groups = [(0, EARLY), (0, SPARSE), (2, EARLY), (1, EARLY), (2, SPARSE), (1, LATE), (0, LATE), (2, LATE), (1, SPARSE)]
 
         def accumulator(g):
             turn, bank = divmod(g, BANKS)
@@ -158,15 +157,6 @@ def tile_moe_rag_lin_silu_kernel(tc, xT, w_words, w_scales, b, gate, offs, out):
             g0 = s0 - PIECE * e
             window = spread[n][:].indirect(entries(s0, s0 + PIECE))
             nc.vector.tensor_tensor(window, y[n][:, s0 : s0 + PIECE], gates[e][:, g0 : g0 + PIECE], MULT)
-
-        def apply_gate(n):
-            nc.vector.tensor_tensor(gated[n][:], y[n][:, 0:PIECE], gates[0][:], MULT)
-
-        def scatter_gated(n):
-            nc.scalar.activation(spread[n][:].indirect(entries(0, PIECE)), gated[n][:], COPY)
-
-        def store(n):
-            nc.sync.dma_start(out=out[P * n : P * (n + 1), :], in_=spread[n][:])
 
         nc.gpsimd.memset(bias_rows[:], 0.0)
         nc.vector.memset(warm_up[:], 0.0)
@@ -215,15 +205,15 @@ def tile_moe_rag_lin_silu_kernel(tc, xT, w_words, w_scales, b, gate, offs, out):
             gather_words(LAST, part)
             gather_last_plane(part)
 
-        for g in range(len(groups)):
+        for g, (n, part) in enumerate(groups):
             for a in range(PASSES):
                 multiply(a, g)
+            if (n, part) == (0, LATE):
+                nc.scalar.activation(spread[0][:].indirect(entries(0, PIECE)), gated[:], COPY)
             activate(g)
-
-        for n in range(N_BLOCKS):
-            scatter(n, EARLY)
-            apply_gate(n)
-            scatter_gated(n)
-        for n in range(N_BLOCKS):
-            scatter(n, LATE)
-            store(n)
+            if (n, part) == (0, SPARSE):
+                nc.vector.tensor_tensor(gated[:], y[0][:, 0:PIECE], gates[0][:], MULT)
+            else:
+                scatter(n, part)
+            if n not in [later for later, rest in groups[g + 1 :]]:
+                nc.sync.dma_start(out=out[P * n : P * (n + 1), :], in_=spread[n][:])

@@ -18,7 +18,8 @@ PLANE_STEP = 4
 SHIFT_ROWS = 112
 RUN = 4
 
-VECTOR_SHARE = (512, 448, 448, 448)
+VECTOR_SHARE = (512, 448, 448)
+LAST_SHARES = (64, 96)
 
 EARLY, SPARSE, LATE = (256, 1, 2 * PIECE), (0, 0, T), (512, 1, T)
 PARTS = (EARLY, SPARSE, LATE)
@@ -41,7 +42,9 @@ def tile_moe_rag_lin_silu_kernel(tc, xT, w_words, w_scales, b, gate, offs, out):
     nc = tc.nc
     with tc.tile_pool(name="keep", bufs=1) as keep, tc.psum_pool(name="psum", bufs=1) as psum:
         offsets = keep.tile([P, T // 16], U16, name="offsets")
-        raw = [keep.tile([P, PACK, T], F32, name="raw%d" % a, align_bytes=64) for a in range(PASSES)]
+        raw = [keep.tile([P, PACK, T], F32, name="raw%d" % a, align_bytes=64) for a in range(LAST)]
+        raw_head = keep.tile([P, PACK, 2 * PIECE], F32, name="raw_head", align_bytes=64)
+        raw_tail = keep.tile([P, PACK, PIECE], F32, name="raw_tail", align_bytes=64)
         grouped = [keep.tile([P, T, PACK], BF16, name="grouped%d" % a, align_bytes=64) for a in range(PASSES)]
         words = [keep.tile([P, T], I32, name="words%d" % a, align_bytes=64) for a in range(PASSES)]
         shared_planes = keep.tile([P, WIDE], U8, name="shared_planes", align_bytes=64)
@@ -51,18 +54,27 @@ def tile_moe_rag_lin_silu_kernel(tc, xT, w_words, w_scales, b, gate, offs, out):
         w_codes = [keep.tile([P, PASSES, 2 * N], U8, name="w_codes%d" % e, align_bytes=64) for e in range(E)]
         w_planes = [keep.tile([P, PASSES, N], U8, name="w_planes%d" % e, align_bytes=64) for e in range(E)]
         bias_rows = keep.tile([P, P * E], F32, name="bias_rows")
+        gate_rows = keep.tile([P, P], F32, name="gate_rows")
+        gate_columns = keep.tile([P, T // P], F32, name="gate_columns")
         identity = keep.tile([P, P], F32, name="identity")
         bias = keep.tile([P, N_BLOCKS, E], F32, name="bias")
-        gates = [keep.tile([P, PIECE * (e + 1)], F32, name="gates%d" % e) for e in range(E)]
+        gates = keep.tile([P, T], F32, name="gates")
         gated = keep.tile([P, PIECE], F32, name="gated")
         warm_up = keep.tile([P, 1], F32, name="warm_up")
         y = [keep.tile([P, T], F32, name="y%d" % n) for n in range(N_BLOCKS)]
         spread = [keep.tile([P, T], F32, name="spread%d" % n) for n in range(N_BLOCKS)]
         banks = [psum.tile([P, 512], F32, name="bank%d" % i) for i in range(BANKS)]
 
-        def load_x(a):
-            rows = xT[a * K_PASS : (a + 1) * K_PASS, :].rearrange("(p j) t -> p j t", j=PACK)
-            nc.sync.dma_start(out=raw[a][:], in_=rows)
+        def load_x(tile, a, t0, t1):
+            rows = xT[a * K_PASS : (a + 1) * K_PASS, t0:t1].rearrange("(p j) t -> p j t", j=PACK)
+            nc.sync.dma_start(out=tile[:], in_=rows)
+
+        def raw_tokens(a, t0, t1):
+            if a < LAST:
+                return raw[a][:, :, t0:t1]
+            if t1 <= 2 * PIECE:
+                return raw_head[:, :, t0:t1]
+            return raw_tail[:, :, t0 - 2 * PIECE : t1 - 2 * PIECE]
 
         def load_scales(e):
             for r in range(4):
@@ -76,12 +88,23 @@ def tile_moe_rag_lin_silu_kernel(tc, xT, w_words, w_scales, b, gate, offs, out):
                 out=w_codes[e][:].bitcast(I32), in_=w_words[e].rearrange("a p c -> p a c").bitcast(I32)
             )
 
-        def load_gate(e):
-            nc.sync.dma_start(out=gates[e][:], in_=gate[0:P, PIECE * e : PIECE * (2 * e + 1)])
+        def turn_bias_and_gate():
+            turned = banks[BANKS - 1]
+            for e in range(E):
+                nc.tensor.transpose(turned[:, P * e : P * (e + 1)], bias_rows[:, e : E * P : E], identity[:])
+            nc.tensor.transpose(turned[:, E * P : (E + 1) * P], gate_rows[:], identity[:])
+            by_block = turned[:, 0 : E * P].rearrange("p (e n) -> p n e", e=E)
+            nc.scalar.activation(bias[:], by_block[:, 0:N_BLOCKS, :], COPY)
+            nc.scalar.activation(gate_columns[:], turned[:, E * P : E * P + T // P], COPY)
+            for bank, (s0, s1) in enumerate(((0, 2 * PIECE), (2 * PIECE, T))):
+                for m in range(s0 // P, s1 // P):
+                    column = gate_columns[:, m : m + 1].to_broadcast([P, P])
+                    nc.tensor.transpose(banks[bank][:, P * m - s0 : P * (m + 1) - s0], column, identity[:])
+                nc.scalar.activation(gates[:, s0:s1], banks[bank][:, 0 : s1 - s0], COPY)
 
         def round_tokens(on_vector, a, t0, t1):
             dst = grouped[a][:, t0:t1, :].rearrange("p (c i) j -> p c j i", i=RUN)
-            src = raw[a][:, :, t0:t1].rearrange("p j (c i) -> p c j i", i=RUN)
+            src = raw_tokens(a, t0, t1).rearrange("p j (c i) -> p c j i", i=RUN)
             if on_vector:
                 nc.vector.tensor_copy(dst, src)
             else:
@@ -154,11 +177,11 @@ def tile_moe_rag_lin_silu_kernel(tc, xT, w_words, w_scales, b, gate, offs, out):
 
         def scatter(n, part):
             s0, e, columns = part
-            g0 = s0 - PIECE * e
             window = spread[n][:].indirect(entries(s0, s0 + PIECE))
-            nc.vector.tensor_tensor(window, y[n][:, s0 : s0 + PIECE], gates[e][:, g0 : g0 + PIECE], MULT)
+            nc.vector.tensor_tensor(window, y[n][:, s0 : s0 + PIECE], gates[:, s0 : s0 + PIECE], MULT)
 
         nc.gpsimd.memset(bias_rows[:], 0.0)
+        nc.gpsimd.memset(gate_rows[:], 0.0)
         nc.vector.memset(warm_up[:], 0.0)
         nc.scalar.activation(warm_up[:], warm_up[:], SILU)
         for e in range(E):
@@ -168,24 +191,24 @@ def tile_moe_rag_lin_silu_kernel(tc, xT, w_words, w_scales, b, gate, offs, out):
         for a in range(1, LAST):
             nc.vector.memset(slot_planes[a][:].bitcast(I32), 0)
 
-        load_x(0)
+        load_x(raw[0], 0, 0, T)
         nc.sync.dma_start(offsets[:], offs)
-        load_x(1)
         nc.sync.dma_start(out=bias_rows[0:N_BLOCKS, :], in_=b.rearrange("(n p) e -> n (p e)", p=P))
-        load_x(2)
+        nc.sync.dma_start(out=gate_rows[0 : T // P, :], in_=gate[0, :].rearrange("(m p) -> m p", p=P))
+        load_x(raw[1], 1, 0, T)
+        load_x(raw[2], 2, 0, T)
+        load_x(raw_head, LAST, 0, 2 * PIECE)
         load_scales(1)
         load_codes(1)
-        load_x(3)
+        load_x(raw_tail, LAST, 2 * PIECE, T)
         load_scales(0)
 
         make_identity(nc, identity[:])
-        turned = banks[BANKS - 1]
-        for e in range(E):
-            nc.tensor.transpose(turned[:, P * e : P * (e + 1)], bias_rows[:, e : E * P : E], identity[:])
-        nc.scalar.activation(bias[:], turned[:, 0 : E * P].rearrange("p (e n) -> p n e", e=E)[:, 0:N_BLOCKS, :], COPY)
 
         for a in range(LAST):
             round_pass(a)
+            if a == 0:
+                turn_bias_and_gate()
             for t0 in range(0, T, PIECE):
                 quantize(a, t0)
             gather_words(a, PARTS[0])
@@ -195,13 +218,18 @@ def tile_moe_rag_lin_silu_kernel(tc, xT, w_words, w_scales, b, gate, offs, out):
                 gather_words(a, part)
 
         load_codes(0)
-        load_gate(0)
-        load_gate(1)
 
-        round_pass(LAST)
-        for t0 in range(0, T, PIECE):
-            quantize(LAST, t0)
-        for part in PARTS:
+        round_tokens(False, LAST, 0, PIECE)
+        round_tokens(False, LAST, PIECE, 2 * PIECE - LAST_SHARES[0])
+        round_tokens(True, LAST, 2 * PIECE - LAST_SHARES[0], 2 * PIECE)
+        quantize(LAST, 0)
+        quantize(LAST, PIECE)
+        round_tokens(False, LAST, 2 * PIECE, T - LAST_SHARES[1])
+        round_tokens(True, LAST, T - LAST_SHARES[1], T)
+        gather_words(LAST, EARLY)
+        quantize(LAST, 2 * PIECE)
+        gather_last_plane(EARLY)
+        for part in PARTS[1:]:
             gather_words(LAST, part)
             gather_last_plane(part)
 
@@ -212,7 +240,7 @@ def tile_moe_rag_lin_silu_kernel(tc, xT, w_words, w_scales, b, gate, offs, out):
                 nc.scalar.activation(spread[0][:].indirect(entries(0, PIECE)), gated[:], COPY)
             activate(g)
             if (n, part) == (0, SPARSE):
-                nc.vector.tensor_tensor(gated[:], y[0][:, 0:PIECE], gates[0][:], MULT)
+                nc.vector.tensor_tensor(gated[:], y[0][:, 0:PIECE], gates[:, 0:PIECE], MULT)
             else:
                 scatter(n, part)
             if n not in [later for later, rest in groups[g + 1 :]]:

@@ -19,11 +19,10 @@ SHIFT_ROWS = 112
 RUN = 4
 
 VECTOR_SHARE = (512, 448, 448)
-LAST_SHARES = (64, 96)
+LAST_SHARES = (64, 128)
 
-EARLY, SPARSE, LATE = (256, 1, 2 * PIECE), (0, 0, T), (512, 1, T)
-PARTS = (EARLY, SPARSE, LATE)
-
+EARLY, LATE, SPARSE = (256, 1, 2 * PIECE), (512, 1, T), (0, 0, T)
+PARTS = (EARLY, LATE, SPARSE)
 
 F32 = mybir.dt.float32
 BF16 = mybir.dt.bfloat16
@@ -48,7 +47,7 @@ def tile_moe_rag_lin_silu_kernel(tc, xT, w_words, w_scales, b, gate, offs, out):
         grouped = [keep.tile([P, T, PACK], BF16, name="grouped%d" % a, align_bytes=64) for a in range(PASSES)]
         words = [keep.tile([P, T], I32, name="words%d" % a, align_bytes=64) for a in range(PASSES)]
         shared_planes = keep.tile([P, WIDE], U8, name="shared_planes", align_bytes=64)
-        last_plane = keep.tile([P, WIDE], U8, name="last_plane", align_bytes=64)
+        last_plane = keep.tile([P, T], U8, name="last_plane", align_bytes=64)
         slot_words = [keep.tile([P, T], U32, name="slot_words%d" % a, align_bytes=64) for a in range(PASSES)]
         slot_planes = [keep.tile([P, T], U8, name="slot_planes%d" % a, align_bytes=64) for a in range(PASSES)]
         w_codes = [keep.tile([P, PASSES, 2 * N], U8, name="w_codes%d" % e, align_bytes=64) for e in range(E)]
@@ -57,9 +56,8 @@ def tile_moe_rag_lin_silu_kernel(tc, xT, w_words, w_scales, b, gate, offs, out):
         gate_rows = keep.tile([P, P], F32, name="gate_rows")
         gate_columns = keep.tile([P, T // P], F32, name="gate_columns")
         identity = keep.tile([P, P], F32, name="identity")
-        bias = keep.tile([P, N_BLOCKS, E], F32, name="bias")
+        bias = [keep.tile([P, E], F32, name="bias%d" % n, tag="bias%d" % n) for n in range(N_BLOCKS)]
         gates = keep.tile([P, T], F32, name="gates")
-        gated = keep.tile([P, PIECE], F32, name="gated")
         warm_up = keep.tile([P, 1], F32, name="warm_up")
         y = [keep.tile([P, T], F32, name="y%d" % n) for n in range(N_BLOCKS)]
         spread = [keep.tile([P, T], F32, name="spread%d" % n) for n in range(N_BLOCKS)]
@@ -93,8 +91,8 @@ def tile_moe_rag_lin_silu_kernel(tc, xT, w_words, w_scales, b, gate, offs, out):
             for e in range(E):
                 nc.tensor.transpose(turned[:, P * e : P * (e + 1)], bias_rows[:, e : E * P : E], identity[:])
             nc.tensor.transpose(turned[:, E * P : (E + 1) * P], gate_rows[:], identity[:])
-            by_block = turned[:, 0 : E * P].rearrange("p (e n) -> p n e", e=E)
-            nc.scalar.activation(bias[:], by_block[:, 0:N_BLOCKS, :], COPY)
+            for n in range(N_BLOCKS):
+                nc.scalar.activation(bias[n][:], turned[:, n : E * P : P], COPY)
             nc.scalar.activation(gate_columns[:], turned[:, E * P : E * P + T // P], COPY)
             for bank, (s0, s1) in enumerate(((0, 2 * PIECE), (2 * PIECE, T))):
                 for m in range(s0 // P, s1 // P):
@@ -152,7 +150,8 @@ def tile_moe_rag_lin_silu_kernel(tc, xT, w_words, w_scales, b, gate, offs, out):
                     in_=slot_planes[0][PLANE_STEP * a : PLANE_STEP * a + SHIFT_ROWS, :].bitcast(I32),
                 )
 
-        groups = [(0, EARLY), (0, SPARSE), (2, EARLY), (1, EARLY), (2, SPARSE), (1, LATE), (0, LATE), (2, LATE), (1, SPARSE)]
+        groups = [(n, EARLY) for n in range(N_BLOCKS)] + [(1, LATE), (2, LATE)]
+        groups = groups + [(0, SPARSE), (1, SPARSE), (2, SPARSE), (0, LATE)]
 
         def accumulator(g):
             turn, bank = divmod(g, BANKS)
@@ -173,7 +172,7 @@ def tile_moe_rag_lin_silu_kernel(tc, xT, w_words, w_scales, b, gate, offs, out):
 
         def activate(g):
             n, (s0, e, columns) = groups[g]
-            nc.scalar.activation(y[n][:, s0 : s0 + PIECE], accumulator(g), SILU, bias=bias[:, n, e : e + 1])
+            nc.scalar.activation(y[n][:, s0 : s0 + PIECE], accumulator(g), SILU, bias=bias[n][:, e : e + 1])
 
         def scatter(n, part):
             s0, e, columns = part
@@ -236,12 +235,12 @@ def tile_moe_rag_lin_silu_kernel(tc, xT, w_words, w_scales, b, gate, offs, out):
         for g, (n, part) in enumerate(groups):
             for a in range(PASSES):
                 multiply(a, g)
-            if (n, part) == (0, LATE):
-                nc.scalar.activation(spread[0][:].indirect(entries(0, PIECE)), gated[:], COPY)
             activate(g)
-            if (n, part) == (0, SPARSE):
+            if (n, part) == (1, SPARSE):
+                gated = keep.tile([P, PIECE], F32, name="gated", tag="bias1")
                 nc.vector.tensor_tensor(gated[:], y[0][:, 0:PIECE], gates[:, 0:PIECE], MULT)
-            else:
+                nc.scalar.activation(spread[0][:].indirect(entries(0, PIECE)), gated[:], COPY)
+            if (n, part) != (0, SPARSE):
                 scatter(n, part)
             if n not in [later for later, rest in groups[g + 1 :]]:
                 nc.sync.dma_start(out=out[P * n : P * (n + 1), :], in_=spread[n][:])

@@ -11,15 +11,14 @@ K_PASS = P * PACK
 PASSES = K // K_PASS
 LAST = PASSES - 1
 N_BLOCKS = N // P
-BANKS = 8
 PIECE = 256
 WIDE = 1024
 PLANE_STEP = 4
 SHIFT_ROWS = 112
 RUN = 4
 
-VECTOR_SHARE = (512, 448, 448)
-LAST_SHARES = (64, 128)
+VECTOR_SHARE = (512, 416)
+HALF = PIECE // 2
 
 EARLY, LATE, SPARSE = (256, 1, 2 * PIECE), (512, 1, T), (0, 0, T)
 PARTS = (EARLY, LATE, SPARSE)
@@ -41,16 +40,16 @@ def tile_moe_rag_lin_silu_kernel(tc, xT, w_words, w_scales, b, gate, offs, out):
     nc = tc.nc
     with tc.tile_pool(name="keep", bufs=1) as keep, tc.psum_pool(name="psum", bufs=1) as psum:
         offsets = keep.tile([P, T // 16], U16, name="offsets")
-        raw = [keep.tile([P, PACK, T], F32, name="raw%d" % a, align_bytes=64) for a in range(LAST)]
-        raw_head = keep.tile([P, PACK, 2 * PIECE], F32, name="raw_head", align_bytes=64)
-        raw_tail = keep.tile([P, PACK, PIECE], F32, name="raw_tail", align_bytes=64)
+        raw = [keep.tile([P, PACK, T], F32, name="raw%d" % a, tag="raw%d" % a, align_bytes=64) for a in range(LAST)]
+        raw_head = keep.tile([P, PACK, 2 * PIECE], F32, name="raw_head", tag="raw_head", align_bytes=64)
+        raw_tail = keep.tile([P, PACK, PIECE], F32, name="raw_tail", tag="raw_tail", align_bytes=64)
         grouped = [keep.tile([P, T, PACK], BF16, name="grouped%d" % a, align_bytes=64) for a in range(PASSES)]
-        words = [keep.tile([P, T], I32, name="words%d" % a, align_bytes=64) for a in range(PASSES)]
-        shared_planes = keep.tile([P, WIDE], U8, name="shared_planes", align_bytes=64)
-        last_plane = keep.tile([P, T], U8, name="last_plane", align_bytes=64)
-        slot_words = [keep.tile([P, T], U32, name="slot_words%d" % a, align_bytes=64) for a in range(PASSES)]
+        words = [keep.tile([P, T], I32, name="words%d" % a, tag="words%d" % a, align_bytes=64) for a in range(PASSES)]
+        planes = keep.tile([P, 3 * T], U8, name="planes", tag="planes", align_bytes=64)
+        slot_words = {}
         slot_planes = [keep.tile([P, T], U8, name="slot_planes%d" % a, align_bytes=64) for a in range(PASSES)]
-        w_codes = [keep.tile([P, PASSES, 2 * N], U8, name="w_codes%d" % e, align_bytes=64) for e in range(E)]
+        w1_codes = [keep.tile([P, 2, 2 * N], U8, name="w1_codes%d" % h, align_bytes=64) for h in range(2)]
+        w0_codes = keep.tile([P, PASSES, 2 * N], U8, name="w0_codes", align_bytes=64)
         w_planes = [keep.tile([P, PASSES, N], U8, name="w_planes%d" % e, align_bytes=64) for e in range(E)]
         bias_rows = keep.tile([P, P * E], F32, name="bias_rows")
         gate_rows = keep.tile([P, P], F32, name="gate_rows")
@@ -58,10 +57,9 @@ def tile_moe_rag_lin_silu_kernel(tc, xT, w_words, w_scales, b, gate, offs, out):
         identity = keep.tile([P, P], F32, name="identity")
         bias = [keep.tile([P, E], F32, name="bias%d" % n, tag="bias%d" % n) for n in range(N_BLOCKS)]
         gates = keep.tile([P, T], F32, name="gates")
-        warm_up = keep.tile([P, 1], F32, name="warm_up")
-        y = [keep.tile([P, T], F32, name="y%d" % n) for n in range(N_BLOCKS)]
-        spread = [keep.tile([P, T], F32, name="spread%d" % n) for n in range(N_BLOCKS)]
-        banks = [psum.tile([P, 512], F32, name="bank%d" % i) for i in range(BANKS)]
+        y = {}
+        gated = [keep.tile([P, PIECE], F32, name="gated%d" % n) for n in range(2)]
+        banks = [psum.tile([P, 512], F32, name="bank%d" % i) for i in range(8)]
 
         def load_x(tile, a, t0, t1):
             rows = xT[a * K_PASS : (a + 1) * K_PASS, t0:t1].rearrange("(p j) t -> p j t", j=PACK)
@@ -81,24 +79,25 @@ def tile_moe_rag_lin_silu_kernel(tc, xT, w_words, w_scales, b, gate, offs, out):
                     in_=w_scales[e, :, r:16:4, :].rearrange("a q n -> q a n").bitcast(I32),
                 )
 
-        def load_codes(e):
-            nc.sync.dma_start(
-                out=w_codes[e][:].bitcast(I32), in_=w_words[e].rearrange("a p c -> p a c").bitcast(I32)
-            )
+        def load_codes(tile, e, a0, a1):
+            nc.sync.dma_start(out=tile[:].bitcast(I32), in_=w_words[e, a0:a1].rearrange("a p c -> p a c").bitcast(I32))
+
+        def w_codes(e, a):
+            return w1_codes[a // 2][:, a % 2, :] if e == 1 else w0_codes[:, a, :]
 
         def turn_bias_and_gate():
-            turned = banks[BANKS - 1]
+            turned = banks[7]
             for e in range(E):
                 nc.tensor.transpose(turned[:, P * e : P * (e + 1)], bias_rows[:, e : E * P : E], identity[:])
             nc.tensor.transpose(turned[:, E * P : (E + 1) * P], gate_rows[:], identity[:])
             for n in range(N_BLOCKS):
                 nc.scalar.activation(bias[n][:], turned[:, n : E * P : P], COPY)
             nc.scalar.activation(gate_columns[:], turned[:, E * P : E * P + T // P], COPY)
-            for bank, (s0, s1) in enumerate(((0, 2 * PIECE), (2 * PIECE, T))):
+            for bank, (s0, s1) in ((banks[6], (0, 2 * PIECE)), (banks[5], (2 * PIECE, T))):
                 for m in range(s0 // P, s1 // P):
                     column = gate_columns[:, m : m + 1].to_broadcast([P, P])
-                    nc.tensor.transpose(banks[bank][:, P * m - s0 : P * (m + 1) - s0], column, identity[:])
-                nc.scalar.activation(gates[:, s0:s1], banks[bank][:, 0 : s1 - s0], COPY)
+                    nc.tensor.transpose(bank[:, P * m - s0 : P * (m + 1) - s0], column, identity[:])
+                nc.scalar.activation(gates[:, s0:s1], bank[:, 0 : s1 - s0], COPY)
 
         def round_tokens(on_vector, a, t0, t1):
             dst = grouped[a][:, t0:t1, :].rearrange("p (c i) j -> p c j i", i=RUN)
@@ -113,82 +112,58 @@ def tile_moe_rag_lin_silu_kernel(tc, xT, w_words, w_scales, b, gate, offs, out):
                 round_tokens(True, a, 0, PIECE)
                 round_tokens(True, a, PIECE, VECTOR_SHARE[a])
                 round_tokens(False, a, VECTOR_SHARE[a], T)
-            else:
+            elif a == 1:
                 cut = PIECE + VECTOR_SHARE[a]
                 round_tokens(True, a, 0, PIECE)
                 round_tokens(False, a, PIECE, 2 * PIECE)
                 round_tokens(True, a, 2 * PIECE, cut)
                 round_tokens(False, a, cut, T)
+            elif a == 2:
+                for t0 in (0, PIECE):
+                    round_tokens(True, a, t0, t0 + HALF)
+                    round_tokens(False, a, t0 + HALF, t0 + PIECE)
+                round_tokens(False, a, 2 * PIECE, T)
+            else:
+                for t0 in range(0, T, PIECE):
+                    round_tokens(False, a, t0, t0 + PIECE)
+
+        def plane_start(a):
+            return T * max(a - 1, 0)
 
         def quantize(a, t0):
-            plane = last_plane if a == LAST else shared_planes
-            first_row = 0 if a == LAST else PLANE_STEP * a
+            first_row = PLANE_STEP if a == 1 else 0
+            c0 = plane_start(a) + t0
             nc.vector.quantize_mx(
                 out=words[a][:, t0 : t0 + PIECE].bitcast(E4M3X4),
-                scales=plane[first_row:P, t0 : t0 + PIECE],
+                scales=planes[first_row:P, c0 : c0 + PIECE],
                 in_=grouped[a][:, t0 : t0 + PIECE, :].rearrange("p t j -> p (t j)"),
             )
 
         def entries(s0, s1):
             return offsets[:, s0 // 16 : s1 // 16]
 
-        def gather_words(a, part):
+        def gather_words(a, part, after=None):
             s0, e, columns = part
-            window = words[a][:, 0:columns].bitcast(U32)
-            nc.vector.tensor_copy(slot_words[a][:, s0 : s0 + PIECE], window.indirect(entries(s0, s0 + PIECE)))
+            name = "slot_words%d_%d" % (a, s0)
+            dst = keep.tile([P, PIECE], U32, name=name, tag=after or name, align_bytes=64)
+            nc.vector.tensor_copy(dst[:], words[a][:, 0:columns].bitcast(U32).indirect(entries(s0, s0 + PIECE)))
+            slot_words[a, part] = dst
+
+        def gather_plane(dst, a):
+            c0 = plane_start(a)
+            nc.vector.tensor_copy(dst[:], planes[:, c0 : c0 + WIDE].indirect(entries(0, T)))
 
         def gather_last_plane(part):
             s0, e, columns = part
-            window = last_plane[:, 0:columns]
+            window = planes[:, plane_start(LAST) : plane_start(LAST) + columns]
             nc.vector.tensor_copy(slot_planes[LAST][:, s0 : s0 + PIECE], window.indirect(entries(s0, s0 + PIECE)))
-
-        def gather_shared_planes():
-            nc.vector.tensor_copy(slot_planes[0][:], shared_planes[:].indirect(entries(0, T)))
-            for a in range(1, LAST):
-                nc.sync.dma_start(
-                    out=slot_planes[a][0:SHIFT_ROWS, :].bitcast(I32),
-                    in_=slot_planes[0][PLANE_STEP * a : PLANE_STEP * a + SHIFT_ROWS, :].bitcast(I32),
-                )
-
-        groups = [(n, EARLY) for n in range(N_BLOCKS)] + [(1, LATE), (2, LATE)]
-        groups = groups + [(0, SPARSE), (1, SPARSE), (2, SPARSE), (0, LATE)]
-
-        def accumulator(g):
-            turn, bank = divmod(g, BANKS)
-            return banks[bank][:, PIECE * turn : PIECE * (turn + 1)]
-
-        def multiply(a, g):
-            n, (s0, e, columns) = groups[g]
-            slots = slice(s0, s0 + PIECE)
-            nc.tensor.matmul_mx(
-                out=accumulator(g),
-                lhsT=w_codes[e][:, a, 2 * P * n : 2 * P * (n + 1)].bitcast(E2M1X4),
-                lhsT_scale=w_planes[e][:, a, P * n : P * (n + 1)],
-                rhs=slot_words[a][:, slots].bitcast(E4M3X4),
-                rhs_scale=slot_planes[a][:, slots],
-                start=(a == 0),
-                stop=(a == LAST),
-            )
-
-        def activate(g):
-            n, (s0, e, columns) = groups[g]
-            nc.scalar.activation(y[n][:, s0 : s0 + PIECE], accumulator(g), SILU, bias=bias[n][:, e : e + 1])
-
-        def scatter(n, part):
-            s0, e, columns = part
-            window = spread[n][:].indirect(entries(s0, s0 + PIECE))
-            nc.vector.tensor_tensor(window, y[n][:, s0 : s0 + PIECE], gates[:, s0 : s0 + PIECE], MULT)
 
         nc.gpsimd.memset(bias_rows[:], 0.0)
         nc.gpsimd.memset(gate_rows[:], 0.0)
-        nc.vector.memset(warm_up[:], 0.0)
-        nc.scalar.activation(warm_up[:], warm_up[:], SILU)
         for e in range(E):
             nc.vector.memset(w_planes[e][:].rearrange("p a n -> p (a n)").bitcast(I32), 0)
-        nc.vector.memset(shared_planes[:].bitcast(I32), 0)
-        nc.vector.memset(last_plane[:].bitcast(I32), 0)
-        for a in range(1, LAST):
-            nc.vector.memset(slot_planes[a][:].bitcast(I32), 0)
+        nc.vector.memset(planes[:].bitcast(I32), 0)
+        nc.vector.memset(slot_planes[1][:].bitcast(I32), 0)
 
         load_x(raw[0], 0, 0, T)
         nc.sync.dma_start(offsets[:], offs)
@@ -198,49 +173,122 @@ def tile_moe_rag_lin_silu_kernel(tc, xT, w_words, w_scales, b, gate, offs, out):
         load_x(raw[2], 2, 0, T)
         load_x(raw_head, LAST, 0, 2 * PIECE)
         load_scales(1)
-        load_codes(1)
+        load_codes(w1_codes[0], 1, 0, 2)
         load_x(raw_tail, LAST, 2 * PIECE, T)
-        load_scales(0)
 
         make_identity(nc, identity[:])
 
-        for a in range(LAST):
-            round_pass(a)
-            if a == 0:
-                turn_bias_and_gate()
+        def quantize_pass(a):
             for t0 in range(0, T, PIECE):
                 quantize(a, t0)
-            gather_words(a, PARTS[0])
-            if a == LAST - 1:
-                gather_shared_planes()
-            for part in PARTS[1:]:
-                gather_words(a, part)
 
-        load_codes(0)
+        round_pass(0)
+        turn_bias_and_gate()
+        quantize_pass(0)
+        for part in PARTS:
+            gather_words(0, part)
 
-        round_tokens(False, LAST, 0, PIECE)
-        round_tokens(False, LAST, PIECE, 2 * PIECE - LAST_SHARES[0])
-        round_tokens(True, LAST, 2 * PIECE - LAST_SHARES[0], 2 * PIECE)
+        round_pass(1)
+        quantize_pass(1)
+        gather_words(1, EARLY)
+        gather_plane(slot_planes[0], 1)
+        nc.sync.dma_start(
+            out=slot_planes[1][0:SHIFT_ROWS, :].bitcast(I32),
+            in_=slot_planes[0][PLANE_STEP : PLANE_STEP + SHIFT_ROWS, :].bitcast(I32),
+        )
+        load_codes(w1_codes[1], 1, 2, PASSES)
+        load_scales(0)
+        load_codes(w0_codes, 0, 0, PASSES)
+        gather_words(1, LATE)
+        gather_words(1, SPARSE)
+
+        round_pass(2)
+        quantize_pass(2)
+        gather_words(2, EARLY, after="raw2")
+        gather_plane(slot_planes[2], 2)
+        gather_words(2, LATE)
+
+        round_pass(LAST)
         quantize(LAST, 0)
         quantize(LAST, PIECE)
-        round_tokens(False, LAST, 2 * PIECE, T - LAST_SHARES[1])
-        round_tokens(True, LAST, T - LAST_SHARES[1], T)
-        gather_words(LAST, EARLY)
-        quantize(LAST, 2 * PIECE)
+        gather_words(2, SPARSE, after="raw_head")
         gather_last_plane(EARLY)
-        for part in PARTS[1:]:
+        quantize(LAST, 2 * PIECE)
+        gather_words(LAST, EARLY, after="raw_tail")
+        for part in (LATE, SPARSE):
             gather_words(LAST, part)
             gather_last_plane(part)
 
-        for g, (n, part) in enumerate(groups):
+        def accumulator(n, part):
+            if part == SPARSE:
+                return banks[n][:, PIECE : 2 * PIECE] if n < 2 else banks[0][:, 0:PIECE]
+            return banks[n if part == EARLY else N_BLOCKS + n][:, 0:PIECE]
+
+        def multiply(a, n, part):
+            s0, e, columns = part
+            slots = slice(s0, s0 + PIECE)
+            nc.tensor.matmul_mx(
+                out=accumulator(n, part),
+                lhsT=w_codes(e, a)[:, 2 * P * n : 2 * P * (n + 1)].bitcast(E2M1X4),
+                lhsT_scale=w_planes[e][:, a, P * n : P * (n + 1)],
+                rhs=slot_words[a, part][:].bitcast(E4M3X4),
+                rhs_scale=slot_planes[a][:, slots],
+                start=(a == 0),
+                stop=(a == LAST),
+            )
+
+        def activate(n, part, after=None):
+            s0, e, columns = part
+            name = "y%d_%d" % (n, s0)
+            y[n, part] = keep.tile([P, PIECE], F32, name=name, tag=after or name)
+            nc.scalar.activation(y[n, part][:], accumulator(n, part), SILU, bias=bias[n][:, e : e + 1])
+
+        for a in range(LAST):
+            for part in (EARLY, LATE):
+                for n in range(N_BLOCKS):
+                    multiply(a, n, part)
+        for part in (EARLY, LATE):
+            for n in range(N_BLOCKS):
+                multiply(LAST, n, part)
+                if (n, part) != (2, LATE):
+                    activate(n, part)
+
+        def sparse_group(n):
             for a in range(PASSES):
-                multiply(a, g)
-            activate(g)
-            if (n, part) == (1, SPARSE):
-                gated = keep.tile([P, PIECE], F32, name="gated", tag="bias1")
-                nc.vector.tensor_tensor(gated[:], y[0][:, 0:PIECE], gates[:, 0:PIECE], MULT)
-                nc.scalar.activation(spread[0][:].indirect(entries(0, PIECE)), gated[:], COPY)
-            if (n, part) != (0, SPARSE):
-                scatter(n, part)
-            if n not in [later for later, rest in groups[g + 1 :]]:
-                nc.sync.dma_start(out=out[P * n : P * (n + 1), :], in_=spread[n][:])
+                multiply(a, n, SPARSE)
+            activate(n, SPARSE)
+
+        spread = {
+            2: keep.tile([P, T], F32, name="spread2", tag="words%d" % LAST, align_bytes=64),
+            0: keep.tile([P, T], F32, name="spread0", tag="planes", align_bytes=64),
+            1: keep.tile([P, T], F32, name="spread1", align_bytes=64),
+        }
+
+        def scatter(n, part):
+            s0, e, columns = part
+            window = spread[n][:].indirect(entries(s0, s0 + PIECE))
+            nc.vector.tensor_tensor(window, y[n, part][:], gates[:, s0 : s0 + PIECE], MULT)
+
+        def scatter_on_scalar(n):
+            nc.vector.tensor_tensor(gated[n][:], y[n, SPARSE][:], gates[:, 0:PIECE], MULT)
+            nc.scalar.activation(spread[n][:].indirect(entries(0, PIECE)), gated[n][:], COPY)
+
+        def store(n):
+            nc.sync.dma_start(out=out[P * n : P * (n + 1), :], in_=spread[n][:])
+
+        sparse_group(0)
+        activate(2, LATE, after="bias0")
+        sparse_group(1)
+        scatter(2, EARLY)
+        scatter(0, EARLY)
+        scatter(1, EARLY)
+        scatter_on_scalar(0)
+        sparse_group(2)
+        scatter(2, LATE)
+        scatter_on_scalar(1)
+        scatter(0, LATE)
+        store(0)
+        scatter(2, SPARSE)
+        store(2)
+        scatter(1, LATE)
+        store(1)

@@ -17,7 +17,7 @@ PLANE_STEP = 4
 SHIFT_ROWS = 112
 RUN = 4
 
-VECTOR_SHARE = (512, 416)
+VECTOR_SHARE = (512, 416, 416)
 HALF = PIECE // 2
 
 EARLY, LATE, SPARSE = (256, 1, 2 * PIECE), (512, 1, T), (0, 0, T)
@@ -45,10 +45,11 @@ def tile_moe_rag_lin_silu_kernel(tc, xT, w_words, w_scales, b, gate, offs, out):
         raw_tail = keep.tile([P, PACK, PIECE], F32, name="raw_tail", tag="raw_tail", align_bytes=64)
         grouped = [keep.tile([P, T, PACK], BF16, name="grouped%d" % a, align_bytes=64) for a in range(PASSES)]
         words = [keep.tile([P, T], I32, name="words%d" % a, tag="words%d" % a, align_bytes=64) for a in range(PASSES)]
-        planes = keep.tile([P, 3 * T], U8, name="planes", tag="planes", align_bytes=64)
+        planes = keep.tile([P, 2 * T], U8, name="planes", tag="planes", align_bytes=64)
         slot_words = {}
         slot_planes = [keep.tile([P, T], U8, name="slot_planes%d" % a, align_bytes=64) for a in range(PASSES)]
-        w1_codes = [keep.tile([P, 2, 2 * N], U8, name="w1_codes%d" % h, align_bytes=64) for h in range(2)]
+        w1_first = keep.tile([P, 1, 2 * N], U8, name="w1_first", align_bytes=64)
+        w1_rest = keep.tile([P, LAST, 2 * N], U8, name="w1_rest", align_bytes=64)
         w0_codes = keep.tile([P, PASSES, 2 * N], U8, name="w0_codes", align_bytes=64)
         w_planes = [keep.tile([P, PASSES, N], U8, name="w_planes%d" % e, align_bytes=64) for e in range(E)]
         bias_rows = keep.tile([P, P * E], F32, name="bias_rows")
@@ -58,7 +59,7 @@ def tile_moe_rag_lin_silu_kernel(tc, xT, w_words, w_scales, b, gate, offs, out):
         bias = [keep.tile([P, E], F32, name="bias%d" % n, tag="bias%d" % n) for n in range(N_BLOCKS)]
         gates = keep.tile([P, T], F32, name="gates")
         y = {}
-        gated = [keep.tile([P, PIECE], F32, name="gated%d" % n) for n in range(2)]
+        gated = keep.tile([P, PIECE], F32, name="gated")
         banks = [psum.tile([P, 512], F32, name="bank%d" % i) for i in range(8)]
 
         def load_x(tile, a, t0, t1):
@@ -83,7 +84,9 @@ def tile_moe_rag_lin_silu_kernel(tc, xT, w_words, w_scales, b, gate, offs, out):
             nc.sync.dma_start(out=tile[:].bitcast(I32), in_=w_words[e, a0:a1].rearrange("a p c -> p a c").bitcast(I32))
 
         def w_codes(e, a):
-            return w1_codes[a // 2][:, a % 2, :] if e == 1 else w0_codes[:, a, :]
+            if e == 0:
+                return w0_codes[:, a, :]
+            return w1_first[:, 0, :] if a == 0 else w1_rest[:, a - 1, :]
 
         def turn_bias_and_gate():
             turned = banks[7]
@@ -112,26 +115,23 @@ def tile_moe_rag_lin_silu_kernel(tc, xT, w_words, w_scales, b, gate, offs, out):
                 round_tokens(True, a, 0, PIECE)
                 round_tokens(True, a, PIECE, VECTOR_SHARE[a])
                 round_tokens(False, a, VECTOR_SHARE[a], T)
-            elif a == 1:
+            elif a < LAST:
                 cut = PIECE + VECTOR_SHARE[a]
                 round_tokens(True, a, 0, PIECE)
                 round_tokens(False, a, PIECE, 2 * PIECE)
                 round_tokens(True, a, 2 * PIECE, cut)
                 round_tokens(False, a, cut, T)
-            elif a == 2:
-                for t0 in (0, PIECE):
-                    round_tokens(True, a, t0, t0 + HALF)
-                    round_tokens(False, a, t0 + HALF, t0 + PIECE)
-                round_tokens(False, a, 2 * PIECE, T)
             else:
-                for t0 in range(0, T, PIECE):
-                    round_tokens(False, a, t0, t0 + PIECE)
+                round_tokens(False, a, 0, PIECE)
+                round_tokens(False, a, PIECE, PIECE + HALF)
+                round_tokens(True, a, PIECE + HALF, 2 * PIECE)
+                round_tokens(False, a, 2 * PIECE, T)
 
         def plane_start(a):
-            return T * max(a - 1, 0)
+            return T if a == LAST else 0
 
         def quantize(a, t0):
-            first_row = PLANE_STEP if a == 1 else 0
+            first_row = 0 if a == LAST else PLANE_STEP * a
             c0 = plane_start(a) + t0
             nc.vector.quantize_mx(
                 out=words[a][:, t0 : t0 + PIECE].bitcast(E4M3X4),
@@ -149,9 +149,13 @@ def tile_moe_rag_lin_silu_kernel(tc, xT, w_words, w_scales, b, gate, offs, out):
             nc.vector.tensor_copy(dst[:], words[a][:, 0:columns].bitcast(U32).indirect(entries(s0, s0 + PIECE)))
             slot_words[a, part] = dst
 
-        def gather_plane(dst, a):
-            c0 = plane_start(a)
-            nc.vector.tensor_copy(dst[:], planes[:, c0 : c0 + WIDE].indirect(entries(0, T)))
+        def gather_shared_planes():
+            nc.vector.tensor_copy(slot_planes[0][:], planes[:, 0:WIDE].indirect(entries(0, T)))
+            for a in range(1, LAST):
+                nc.sync.dma_start(
+                    out=slot_planes[a][0:SHIFT_ROWS, :].bitcast(I32),
+                    in_=slot_planes[0][PLANE_STEP * a : PLANE_STEP * a + SHIFT_ROWS, :].bitcast(I32),
+                )
 
         def gather_last_plane(part):
             s0, e, columns = part
@@ -163,7 +167,8 @@ def tile_moe_rag_lin_silu_kernel(tc, xT, w_words, w_scales, b, gate, offs, out):
         for e in range(E):
             nc.vector.memset(w_planes[e][:].rearrange("p a n -> p (a n)").bitcast(I32), 0)
         nc.vector.memset(planes[:].bitcast(I32), 0)
-        nc.vector.memset(slot_planes[1][:].bitcast(I32), 0)
+        for a in range(1, LAST):
+            nc.vector.memset(slot_planes[a][:].bitcast(I32), 0)
 
         load_x(raw[0], 0, 0, T)
         nc.sync.dma_start(offsets[:], offs)
@@ -173,8 +178,9 @@ def tile_moe_rag_lin_silu_kernel(tc, xT, w_words, w_scales, b, gate, offs, out):
         load_x(raw[2], 2, 0, T)
         load_x(raw_head, LAST, 0, 2 * PIECE)
         load_scales(1)
-        load_codes(w1_codes[0], 1, 0, 2)
+        load_codes(w1_first, 1, 0, 1)
         load_x(raw_tail, LAST, 2 * PIECE, T)
+        load_codes(w1_rest, 1, 1, PASSES)
 
         make_identity(nc, identity[:])
 
@@ -182,31 +188,19 @@ def tile_moe_rag_lin_silu_kernel(tc, xT, w_words, w_scales, b, gate, offs, out):
             for t0 in range(0, T, PIECE):
                 quantize(a, t0)
 
-        round_pass(0)
-        turn_bias_and_gate()
-        quantize_pass(0)
-        for part in PARTS:
-            gather_words(0, part)
-
-        round_pass(1)
-        quantize_pass(1)
-        gather_words(1, EARLY)
-        gather_plane(slot_planes[0], 1)
-        nc.sync.dma_start(
-            out=slot_planes[1][0:SHIFT_ROWS, :].bitcast(I32),
-            in_=slot_planes[0][PLANE_STEP : PLANE_STEP + SHIFT_ROWS, :].bitcast(I32),
-        )
-        load_codes(w1_codes[1], 1, 2, PASSES)
-        load_scales(0)
-        load_codes(w0_codes, 0, 0, PASSES)
-        gather_words(1, LATE)
-        gather_words(1, SPARSE)
-
-        round_pass(2)
-        quantize_pass(2)
-        gather_words(2, EARLY, after="raw2")
-        gather_plane(slot_planes[2], 2)
-        gather_words(2, LATE)
+        for a in range(LAST):
+            round_pass(a)
+            if a == 0:
+                turn_bias_and_gate()
+            quantize_pass(a)
+            gather_words(a, EARLY)
+            if a == LAST - 1:
+                gather_shared_planes()
+                load_scales(0)
+                load_codes(w0_codes, 0, 0, PASSES)
+            gather_words(a, LATE)
+            if a < LAST - 1:
+                gather_words(a, SPARSE)
 
         round_pass(LAST)
         quantize(LAST, 0)
@@ -259,9 +253,9 @@ def tile_moe_rag_lin_silu_kernel(tc, xT, w_words, w_scales, b, gate, offs, out):
             activate(n, SPARSE)
 
         spread = {
-            2: keep.tile([P, T], F32, name="spread2", tag="words%d" % LAST, align_bytes=64),
+            1: keep.tile([P, T], F32, name="spread1", tag="words%d" % LAST, align_bytes=64),
             0: keep.tile([P, T], F32, name="spread0", tag="planes", align_bytes=64),
-            1: keep.tile([P, T], F32, name="spread1", align_bytes=64),
+            2: keep.tile([P, T], F32, name="spread2", align_bytes=64),
         }
 
         def scatter(n, part):
@@ -270,8 +264,8 @@ def tile_moe_rag_lin_silu_kernel(tc, xT, w_words, w_scales, b, gate, offs, out):
             nc.vector.tensor_tensor(window, y[n, part][:], gates[:, s0 : s0 + PIECE], MULT)
 
         def scatter_on_scalar(n):
-            nc.vector.tensor_tensor(gated[n][:], y[n, SPARSE][:], gates[:, 0:PIECE], MULT)
-            nc.scalar.activation(spread[n][:].indirect(entries(0, PIECE)), gated[n][:], COPY)
+            nc.vector.tensor_tensor(gated[:], y[n, SPARSE][:], gates[:, 0:PIECE], MULT)
+            nc.scalar.activation(spread[n][:].indirect(entries(0, PIECE)), gated[:], COPY)
 
         def store(n):
             nc.sync.dma_start(out=out[P * n : P * (n + 1), :], in_=spread[n][:])
@@ -279,16 +273,16 @@ def tile_moe_rag_lin_silu_kernel(tc, xT, w_words, w_scales, b, gate, offs, out):
         sparse_group(0)
         activate(2, LATE, after="bias0")
         sparse_group(1)
-        scatter(2, EARLY)
-        scatter(0, EARLY)
-        scatter(1, EARLY)
-        scatter_on_scalar(0)
         sparse_group(2)
+        scatter(1, EARLY)
+        scatter(0, EARLY)
+        scatter(2, EARLY)
+        scatter(1, LATE)
+        scatter_on_scalar(0)
         scatter(2, LATE)
-        scatter_on_scalar(1)
+        scatter(1, SPARSE)
+        store(1)
         scatter(0, LATE)
         store(0)
         scatter(2, SPARSE)
         store(2)
-        scatter(1, LATE)
-        store(1)

@@ -215,8 +215,10 @@ def tile_moe_rag_lin_silu_kernel(tc, xT, w_words, w_scales, b, gate, offs, out):
 
         def accumulator(n, part):
             if part == SPARSE:
-                return banks[n][:, PIECE : 2 * PIECE] if n < 2 else banks[0][:, 0:PIECE]
+                return banks[2 * N_BLOCKS + n % 2][:, PIECE * (n // 2) : PIECE * (n // 2 + 1)]
             return banks[n if part == EARLY else N_BLOCKS + n][:, 0:PIECE]
+
+        pass_order = {EARLY: (0, 1, 2, 3), LATE: (0, 3, 1, 2), SPARSE: (3, 0, 1, 2)}
 
         def multiply(a, n, part):
             s0, e, columns = part
@@ -227,8 +229,8 @@ def tile_moe_rag_lin_silu_kernel(tc, xT, w_words, w_scales, b, gate, offs, out):
                 lhsT_scale=w_planes[e][:, a, P * n : P * (n + 1)],
                 rhs=slot_words[a, part][:].bitcast(E4M3X4),
                 rhs_scale=slot_planes[a][:, slots],
-                start=(a == 0),
-                stop=(a == LAST),
+                start=(a == pass_order[part][0]),
+                stop=(a == pass_order[part][LAST]),
             )
 
         def activate(n, part, after=None):
@@ -237,19 +239,21 @@ def tile_moe_rag_lin_silu_kernel(tc, xT, w_words, w_scales, b, gate, offs, out):
             y[n, part] = keep.tile([P, PIECE], F32, name=name, tag=after or name)
             nc.scalar.activation(y[n, part][:], accumulator(n, part), SILU, bias=bias[n][:, e : e + 1])
 
-        for a in range(LAST):
-            for part in (EARLY, LATE):
-                for n in range(N_BLOCKS):
-                    multiply(a, n, part)
+        def finish_group(n, part, first):
+            for a in pass_order[part][first:]:
+                multiply(a, n, part)
+
         for part in (EARLY, LATE):
             for n in range(N_BLOCKS):
-                multiply(LAST, n, part)
+                multiply(0, n, part)
+        for part in (EARLY, LATE):
+            for n in range(N_BLOCKS):
+                finish_group(n, part, 1)
                 if (n, part) != (2, LATE):
                     activate(n, part)
 
         def sparse_group(n):
-            for a in range(PASSES):
-                multiply(a, n, SPARSE)
+            finish_group(n, SPARSE, 0)
             activate(n, SPARSE)
 
         spread = {

@@ -257,8 +257,8 @@ def tile_moe_rag_lin_silu_kernel(tc, xT, w_words, w_scales, b, gate, offs, out):
             activate(n, SPARSE)
 
         spread = {
-            1: keep.tile([P, T], F32, name="spread1", tag="words%d" % LAST, align_bytes=64),
-            0: keep.tile([P, T], F32, name="spread0", tag="planes", align_bytes=64),
+            0: keep.tile([P, T], F32, name="spread0", tag="words%d" % LAST, align_bytes=64),
+            1: keep.tile([P, T], F32, name="spread1", tag="planes", align_bytes=64),
             2: keep.tile([P, T], F32, name="spread2", align_bytes=64),
         }
 
@@ -278,8 +278,8 @@ def tile_moe_rag_lin_silu_kernel(tc, xT, w_words, w_scales, b, gate, offs, out):
         activate(2, LATE, after="bias0")
         sparse_group(1)
         sparse_group(2)
-        scatter(1, EARLY)
         scatter(0, EARLY)
+        scatter(1, EARLY)
         scatter(2, EARLY)
         scatter(1, LATE)
         scatter_on_scalar(0)

@@ -16,12 +16,10 @@ WIDE = 1024
 PLANE_STEP = 4
 SHIFT_ROWS = 112
 RUN = 4
-
 VECTOR_SHARE = (512, 416, 416)
-HALF = PIECE // 2
+LAST_SHARE = 128
 
 EARLY, LATE, SPARSE = (256, 1, 2 * PIECE), (512, 1, T), (0, 0, T)
-PARTS = (EARLY, LATE, SPARSE)
 
 F32 = mybir.dt.float32
 BF16 = mybir.dt.bfloat16
@@ -39,136 +37,49 @@ MULT = mybir.AluOpType.mult
 def tile_moe_rag_lin_silu_kernel(tc, xT, w_words, w_scales, b, gate, offs, out):
     nc = tc.nc
     with tc.tile_pool(name="keep", bufs=1) as keep, tc.psum_pool(name="psum", bufs=1) as psum:
+
+        def sbuf(name, shape, dtype, over=None):
+            return keep.tile(shape, dtype, name=name, tag=over or name, align_bytes=64)
+
         offsets = keep.tile([P, T // 16], U16, name="offsets")
-        raw = [keep.tile([P, PACK, T], F32, name="raw%d" % a, tag="raw%d" % a, align_bytes=64) for a in range(LAST)]
-        raw_head = keep.tile([P, PACK, 2 * PIECE], F32, name="raw_head", tag="raw_head", align_bytes=64)
-        raw_tail = keep.tile([P, PACK, PIECE], F32, name="raw_tail", tag="raw_tail", align_bytes=64)
-        grouped = [keep.tile([P, T, PACK], BF16, name="grouped%d" % a, align_bytes=64) for a in range(PASSES)]
-        words = [keep.tile([P, T], I32, name="words%d" % a, tag="words%d" % a, align_bytes=64) for a in range(PASSES)]
-        planes = keep.tile([P, 2 * T], U8, name="planes", tag="planes", align_bytes=64)
+        raw = [sbuf("raw%d" % a, [P, PACK, T], F32) for a in range(LAST)]
+        raw_head = sbuf("raw_head", [P, PACK, 2 * PIECE], F32)
+        raw_tail = sbuf("raw_tail", [P, PACK, PIECE], F32)
+        grouped = [sbuf("grouped%d" % a, [P, T, PACK], BF16) for a in range(PASSES)]
+        words = [sbuf("words%d" % a, [P, T], I32) for a in range(PASSES)]
+        planes = sbuf("planes", [P, 2 * T], U8)
         slot_words = {}
-        slot_planes = [keep.tile([P, T], U8, name="slot_planes%d" % a, align_bytes=64) for a in range(PASSES)]
-        w1_first = keep.tile([P, 1, 2 * N], U8, name="w1_first", align_bytes=64)
-        w1_rest = keep.tile([P, LAST, 2 * N], U8, name="w1_rest", align_bytes=64)
-        w0_codes = keep.tile([P, PASSES, 2 * N], U8, name="w0_codes", align_bytes=64)
-        w_planes = [keep.tile([P, PASSES, N], U8, name="w_planes%d" % e, align_bytes=64) for e in range(E)]
-        bias_rows = keep.tile([P, P * E], F32, name="bias_rows")
-        gate_rows = keep.tile([P, P], F32, name="gate_rows")
-        gate_columns = keep.tile([P, T // P], F32, name="gate_columns")
-        identity = keep.tile([P, P], F32, name="identity")
-        bias = [keep.tile([P, E], F32, name="bias%d" % n, tag="bias%d" % n) for n in range(N_BLOCKS)]
-        gates = keep.tile([P, T], F32, name="gates")
-        y = {}
-        gated = keep.tile([P, PIECE], F32, name="gated")
+        slot_planes = [sbuf("slot_planes%d" % a, [P, T], U8) for a in range(PASSES)]
+        w_first = sbuf("w_first", [P, E, 2 * N], U8)
+        w_rest = [sbuf("w_rest%d" % e, [P, LAST, 2 * N], U8) for e in range(E)]
+        w_planes = sbuf("w_planes", [P, E * PASSES, N], U8)
+        bias_rows = sbuf("bias_rows", [P, P * E], F32)
+        gate_rows = sbuf("gate_rows", [P, P], F32)
+        gate_columns = sbuf("gate_columns", [P, T // P], F32)
+        identity = sbuf("identity", [P, P], F32)
+        bias_dense = sbuf("bias_dense", [P, N_BLOCKS], F32)
+        bias_sparse = sbuf("bias_sparse", [P, N_BLOCKS - 1], F32)
+        bias_sparse_last = sbuf("bias_sparse_last", [P, 1], F32)
+        gates = sbuf("gates", [P, T], F32)
+        gated = sbuf("gated", [P, PIECE], F32)
         banks = [psum.tile([P, 512], F32, name="bank%d" % i) for i in range(8)]
+
+        nc.vector.memset(w_planes[:].rearrange("p a n -> p (a n)").bitcast(I32), 0)
+        nc.gpsimd.memset(bias_rows[:], 0.0)
+        nc.gpsimd.memset(gate_rows[:], 0.0)
+        nc.vector.memset(planes[:].bitcast(I32), 0)
+        for a in range(1, LAST):
+            nc.vector.memset(slot_planes[a][:].bitcast(I32), 0)
+        make_identity(nc, identity[:])
+        for r in range(4):
+            nc.gpsimd.dma_start(
+                out=w_planes[r:P:32, :, :].bitcast(I32),
+                in_=w_scales[:, :, r:16:4, :].rearrange("e a q n -> q (e a) n").bitcast(I32),
+            )
 
         def load_x(tile, a, t0, t1):
             rows = xT[a * K_PASS : (a + 1) * K_PASS, t0:t1].rearrange("(p j) t -> p j t", j=PACK)
             nc.sync.dma_start(out=tile[:], in_=rows)
-
-        def raw_tokens(a, t0, t1):
-            if a < LAST:
-                return raw[a][:, :, t0:t1]
-            if t1 <= 2 * PIECE:
-                return raw_head[:, :, t0:t1]
-            return raw_tail[:, :, t0 - 2 * PIECE : t1 - 2 * PIECE]
-
-        def load_scales(e):
-            for r in range(4):
-                nc.sync.dma_start(
-                    out=w_planes[e][r:P:32, :, :].bitcast(I32),
-                    in_=w_scales[e, :, r:16:4, :].rearrange("a q n -> q a n").bitcast(I32),
-                )
-
-        def load_codes(tile, e, a0, a1):
-            nc.sync.dma_start(out=tile[:].bitcast(I32), in_=w_words[e, a0:a1].rearrange("a p c -> p a c").bitcast(I32))
-
-        def w_codes(e, a):
-            if e == 0:
-                return w0_codes[:, a, :]
-            return w1_first[:, 0, :] if a == 0 else w1_rest[:, a - 1, :]
-
-        def turn_bias_and_gate():
-            turned = banks[7]
-            for e in range(E):
-                nc.tensor.transpose(turned[:, P * e : P * (e + 1)], bias_rows[:, e : E * P : E], identity[:])
-            nc.tensor.transpose(turned[:, E * P : (E + 1) * P], gate_rows[:], identity[:])
-            for n in range(N_BLOCKS):
-                nc.scalar.activation(bias[n][:], turned[:, n : E * P : P], COPY)
-            nc.scalar.activation(gate_columns[:], turned[:, E * P : E * P + T // P], COPY)
-            for bank, (s0, s1) in ((banks[6], (0, 2 * PIECE)), (banks[5], (2 * PIECE, T))):
-                for m in range(s0 // P, s1 // P):
-                    column = gate_columns[:, m : m + 1].to_broadcast([P, P])
-                    nc.tensor.transpose(bank[:, P * m - s0 : P * (m + 1) - s0], column, identity[:])
-                nc.scalar.activation(gates[:, s0:s1], bank[:, 0 : s1 - s0], COPY)
-
-        def round_tokens(on_vector, a, t0, t1):
-            dst = grouped[a][:, t0:t1, :].rearrange("p (c i) j -> p c j i", i=RUN)
-            src = raw_tokens(a, t0, t1).rearrange("p j (c i) -> p c j i", i=RUN)
-            if on_vector:
-                nc.vector.tensor_copy(dst, src)
-            else:
-                nc.scalar.activation(dst, src, COPY)
-
-        def round_pass(a):
-            if a == 0:
-                round_tokens(True, a, 0, PIECE)
-                round_tokens(True, a, PIECE, VECTOR_SHARE[a])
-                round_tokens(False, a, VECTOR_SHARE[a], T)
-            elif a < LAST:
-                cut = PIECE + VECTOR_SHARE[a]
-                round_tokens(True, a, 0, PIECE)
-                round_tokens(False, a, PIECE, 2 * PIECE)
-                round_tokens(True, a, 2 * PIECE, cut)
-                round_tokens(False, a, cut, T)
-            else:
-                round_tokens(False, a, 0, PIECE)
-                round_tokens(False, a, PIECE, PIECE + HALF)
-                round_tokens(True, a, PIECE + HALF, 2 * PIECE)
-                round_tokens(False, a, 2 * PIECE, T)
-
-        def plane_start(a):
-            return T if a == LAST else 0
-
-        def quantize(a, t0):
-            first_row = 0 if a == LAST else PLANE_STEP * a
-            c0 = plane_start(a) + t0
-            nc.vector.quantize_mx(
-                out=words[a][:, t0 : t0 + PIECE].bitcast(E4M3X4),
-                scales=planes[first_row:P, c0 : c0 + PIECE],
-                in_=grouped[a][:, t0 : t0 + PIECE, :].rearrange("p t j -> p (t j)"),
-            )
-
-        def entries(s0, s1):
-            return offsets[:, s0 // 16 : s1 // 16]
-
-        def gather_words(a, part, after=None):
-            s0, e, columns = part
-            name = "slot_words%d_%d" % (a, s0)
-            dst = keep.tile([P, PIECE], U32, name=name, tag=after or name, align_bytes=64)
-            nc.vector.tensor_copy(dst[:], words[a][:, 0:columns].bitcast(U32).indirect(entries(s0, s0 + PIECE)))
-            slot_words[a, part] = dst
-
-        def gather_shared_planes():
-            nc.vector.tensor_copy(slot_planes[0][:], planes[:, 0:WIDE].indirect(entries(0, T)))
-            for a in range(1, LAST):
-                nc.sync.dma_start(
-                    out=slot_planes[a][0:SHIFT_ROWS, :].bitcast(I32),
-                    in_=slot_planes[0][PLANE_STEP * a : PLANE_STEP * a + SHIFT_ROWS, :].bitcast(I32),
-                )
-
-        def gather_last_plane(part):
-            s0, e, columns = part
-            window = planes[:, plane_start(LAST) : plane_start(LAST) + columns]
-            nc.vector.tensor_copy(slot_planes[LAST][:, s0 : s0 + PIECE], window.indirect(entries(s0, s0 + PIECE)))
-
-        nc.gpsimd.memset(bias_rows[:], 0.0)
-        nc.gpsimd.memset(gate_rows[:], 0.0)
-        for e in range(E):
-            nc.vector.memset(w_planes[e][:].rearrange("p a n -> p (a n)").bitcast(I32), 0)
-        nc.vector.memset(planes[:].bitcast(I32), 0)
-        for a in range(1, LAST):
-            nc.vector.memset(slot_planes[a][:].bitcast(I32), 0)
 
         load_x(raw[0], 0, 0, T)
         nc.sync.dma_start(offsets[:], offs)
@@ -177,116 +88,152 @@ def tile_moe_rag_lin_silu_kernel(tc, xT, w_words, w_scales, b, gate, offs, out):
         load_x(raw[1], 1, 0, T)
         load_x(raw[2], 2, 0, T)
         load_x(raw_head, LAST, 0, 2 * PIECE)
-        load_scales(1)
-        load_codes(w1_first, 1, 0, 1)
+        nc.sync.dma_start(out=w_first[:].bitcast(I32), in_=w_words[:, 0].rearrange("e p c -> p e c").bitcast(I32))
         load_x(raw_tail, LAST, 2 * PIECE, T)
-        load_codes(w1_rest, 1, 1, PASSES)
+        for e in (1, 0):
+            nc.sync.dma_start(
+                out=w_rest[e][:].bitcast(I32), in_=w_words[e, 1:PASSES].rearrange("a p c -> p a c").bitcast(I32)
+            )
 
-        make_identity(nc, identity[:])
+        def turn_bias_and_gate():
+            turned = banks[7]
+            for e in range(E):
+                nc.tensor.transpose(turned[:, P * e : P * (e + 1)], bias_rows[:, e : E * P : E], identity[:])
+            nc.tensor.transpose(turned[:, E * P : (E + 1) * P], gate_rows[:], identity[:])
+            nc.scalar.activation(gate_columns[:], turned[:, E * P : E * P + T // P], COPY)
+            nc.scalar.activation(bias_dense[:], turned[:, P : P + N_BLOCKS], COPY)
+            nc.scalar.activation(bias_sparse[:], turned[:, 0 : N_BLOCKS - 1], COPY)
+            nc.scalar.activation(bias_sparse_last[:], turned[:, N_BLOCKS - 1 : N_BLOCKS], COPY)
+            for bank, (s0, s1) in ((banks[6], (0, 2 * PIECE)), (banks[5], (2 * PIECE, T))):
+                for m in range(s0 // P, s1 // P):
+                    column = gate_columns[:, m : m + 1].to_broadcast([P, P])
+                    nc.tensor.transpose(bank[:, P * m - s0 : P * (m + 1) - s0], column, identity[:])
+                nc.scalar.activation(gates[:, s0:s1], bank[:, 0 : s1 - s0], COPY)
 
-        def quantize_pass(a):
-            for t0 in range(0, T, PIECE):
-                quantize(a, t0)
+        def round_tokens(on_vector, a, t0, t1):
+            if a < LAST:
+                src = raw[a][:, :, t0:t1]
+            elif t1 <= 2 * PIECE:
+                src = raw_head[:, :, t0:t1]
+            else:
+                src = raw_tail[:, :, t0 - 2 * PIECE : t1 - 2 * PIECE]
+            src = src.rearrange("p j (c i) -> p c j i", i=RUN)
+            dst = grouped[a][:, t0:t1, :].rearrange("p (c i) j -> p c j i", i=RUN)
+            if on_vector:
+                nc.vector.tensor_copy(dst, src)
+            else:
+                nc.scalar.activation(dst, src, COPY)
+
+        def quantize(a, t0):
+            row, column = (0, T + t0) if a == LAST else (PLANE_STEP * a, t0)
+            nc.vector.quantize_mx(
+                out=words[a][:, t0 : t0 + PIECE].bitcast(E4M3X4),
+                scales=planes[row:P, column : column + PIECE],
+                in_=grouped[a][:, t0 : t0 + PIECE, :].rearrange("p t j -> p (t j)"),
+            )
+
+        def entries(s0, count=PIECE):
+            return offsets[:, s0 // 16 : (s0 + count) // 16]
+
+        def gather_words(a, part, over=None):
+            s0, e, columns = part
+            slot_words[a, part] = sbuf("slot_words%d_%d" % (a, s0), [P, PIECE], U32, over)
+            nc.vector.tensor_copy(slot_words[a, part][:], words[a][:, 0:columns].bitcast(U32).indirect(entries(s0)))
+
+        def gather_last_plane(part):
+            s0, e, columns = part
+            nc.vector.tensor_copy(slot_planes[LAST][:, s0 : s0 + PIECE], planes[:, T : T + columns].indirect(entries(s0)))
 
         for a in range(LAST):
-            round_pass(a)
+            round_tokens(True, a, 0, PIECE)
             if a == 0:
+                round_tokens(True, a, PIECE, VECTOR_SHARE[a])
+                round_tokens(False, a, VECTOR_SHARE[a], T)
                 turn_bias_and_gate()
-            quantize_pass(a)
+            else:
+                cut = PIECE + VECTOR_SHARE[a]
+                round_tokens(False, a, PIECE, 2 * PIECE)
+                round_tokens(True, a, 2 * PIECE, cut)
+                round_tokens(False, a, cut, T)
+            for t0 in range(0, T, PIECE):
+                quantize(a, t0)
             gather_words(a, EARLY)
             if a == LAST - 1:
-                gather_shared_planes()
-                load_scales(0)
-                load_codes(w0_codes, 0, 0, PASSES)
-            gather_words(a, LATE)
+                nc.vector.tensor_copy(slot_planes[0][:], planes[:, 0:WIDE].indirect(entries(0, T)))
+                for moved in range(1, LAST):
+                    row = PLANE_STEP * moved
+                    nc.sync.dma_start(
+                        out=slot_planes[moved][0:SHIFT_ROWS, :].bitcast(I32),
+                        in_=slot_planes[0][row : row + SHIFT_ROWS, :].bitcast(I32),
+                    )
+            gather_words(a, SPARSE)
             if a < LAST - 1:
-                gather_words(a, SPARSE)
+                gather_words(a, LATE)
 
-        round_pass(LAST)
+        cut = 2 * PIECE - LAST_SHARE
+        round_tokens(False, LAST, 0, PIECE)
+        round_tokens(False, LAST, PIECE, cut)
+        round_tokens(True, LAST, cut, 2 * PIECE)
+        round_tokens(False, LAST, 2 * PIECE, T)
         quantize(LAST, 0)
         quantize(LAST, PIECE)
-        gather_words(2, SPARSE, after="raw_head")
+        gather_words(LAST - 1, LATE, over="raw_head")
         gather_last_plane(EARLY)
         quantize(LAST, 2 * PIECE)
-        gather_words(LAST, EARLY, after="raw_tail")
-        for part in (LATE, SPARSE):
+        gather_words(LAST, EARLY, over="raw_tail")
+        for part in (SPARSE, LATE):
             gather_words(LAST, part)
             gather_last_plane(part)
 
-        def accumulator(n, part):
-            if part == SPARSE:
-                return banks[2 * N_BLOCKS + n % 2][:, PIECE * (n // 2) : PIECE * (n // 2 + 1)]
-            return banks[n if part == EARLY else N_BLOCKS + n][:, 0:PIECE]
+        groups = [(2, EARLY), (0, SPARSE), (1, EARLY), (2, SPARSE), (0, EARLY), (2, LATE), (1, LATE), (0, LATE), (1, SPARSE)]
+        sums = {g: banks[i % 8][:, PIECE * (i // 8) : PIECE * (i // 8 + 1)] for i, g in enumerate(groups)}
+        y = {}
 
-        pass_order = {EARLY: (0, 1, 2, 3), LATE: (0, 3, 1, 2), SPARSE: (3, 0, 1, 2)}
-
-        def multiply(a, n, part):
-            s0, e, columns = part
-            slots = slice(s0, s0 + PIECE)
+        def multiply(a, group):
+            n, (s0, e, columns) = group
+            codes = w_first[:, e, :] if a == 0 else w_rest[e][:, a - 1, :]
             nc.tensor.matmul_mx(
-                out=accumulator(n, part),
-                lhsT=w_codes(e, a)[:, 2 * P * n : 2 * P * (n + 1)].bitcast(E2M1X4),
-                lhsT_scale=w_planes[e][:, a, P * n : P * (n + 1)],
-                rhs=slot_words[a, part][:].bitcast(E4M3X4),
-                rhs_scale=slot_planes[a][:, slots],
-                start=(a == pass_order[part][0]),
-                stop=(a == pass_order[part][LAST]),
+                out=sums[group],
+                lhsT=codes[:, 2 * P * n : 2 * P * (n + 1)].bitcast(E2M1X4),
+                lhsT_scale=w_planes[:, PASSES * e + a, P * n : P * (n + 1)],
+                rhs=slot_words[a, group[1]][:].bitcast(E4M3X4),
+                rhs_scale=slot_planes[a][:, s0 : s0 + PIECE],
+                start=(a == 0),
+                stop=(a == LAST),
             )
 
-        def activate(n, part, after=None):
-            s0, e, columns = part
-            name = "y%d_%d" % (n, s0)
-            y[n, part] = keep.tile([P, PIECE], F32, name=name, tag=after or name)
-            nc.scalar.activation(y[n, part][:], accumulator(n, part), SILU, bias=bias[n][:, e : e + 1])
+        def activate(group):
+            n, (s0, e, columns) = group
+            if e == 1:
+                bias = bias_dense[:, n : n + 1]
+            elif n < N_BLOCKS - 1:
+                bias = bias_sparse[:, n : n + 1]
+            else:
+                bias = bias_sparse_last[:]
+            y[group] = sbuf("y%d_%d" % (n, s0), [P, PIECE], F32)
+            nc.scalar.activation(y[group][:], sums[group], SILU, bias=bias)
 
-        def finish_group(n, part, first):
-            for a in pass_order[part][first:]:
-                multiply(a, n, part)
-
-        for part in (EARLY, LATE):
-            for n in range(N_BLOCKS):
-                multiply(0, n, part)
-        for part in (EARLY, LATE):
-            for n in range(N_BLOCKS):
-                finish_group(n, part, 1)
-                if (n, part) != (2, LATE):
-                    activate(n, part)
-
-        def sparse_group(n):
-            finish_group(n, SPARSE, 0)
-            activate(n, SPARSE)
+        for group in groups[:8]:
+            multiply(0, group)
+        for i, group in enumerate(groups):
+            for a in range(0 if i == 8 else 1, PASSES):
+                multiply(a, group)
+            activate(group)
 
         spread = {
-            0: keep.tile([P, T], F32, name="spread0", tag="words%d" % LAST, align_bytes=64),
-            1: keep.tile([P, T], F32, name="spread1", tag="planes", align_bytes=64),
-            2: keep.tile([P, T], F32, name="spread2", align_bytes=64),
+            0: sbuf("spread0", [P, T], F32, over="bias_sparse_last"),
+            1: sbuf("spread1", [P, T], F32, over="words%d" % LAST),
+            2: sbuf("spread2", [P, T], F32, over="planes"),
         }
-
-        def scatter(n, part):
-            s0, e, columns = part
-            window = spread[n][:].indirect(entries(s0, s0 + PIECE))
-            nc.vector.tensor_tensor(window, y[n, part][:], gates[:, s0 : s0 + PIECE], MULT)
-
-        def scatter_on_scalar(n):
-            nc.vector.tensor_tensor(gated[:], y[n, SPARSE][:], gates[:, 0:PIECE], MULT)
-            nc.scalar.activation(spread[n][:].indirect(entries(0, PIECE)), gated[:], COPY)
-
-        def store(n):
-            nc.sync.dma_start(out=out[P * n : P * (n + 1), :], in_=spread[n][:])
-
-        sparse_group(0)
-        activate(2, LATE, after="bias0")
-        sparse_group(1)
-        sparse_group(2)
-        scatter(0, EARLY)
-        scatter(1, EARLY)
-        scatter(2, EARLY)
-        scatter(1, LATE)
-        scatter_on_scalar(0)
-        scatter(2, LATE)
-        scatter(1, SPARSE)
-        store(1)
-        scatter(0, LATE)
-        store(0)
-        scatter(2, SPARSE)
-        store(2)
+        left = {n: 3 for n in range(N_BLOCKS)}
+        for group in groups:
+            n, (s0, e, columns) = group
+            window = spread[n][:].indirect(entries(s0))
+            if group == (0, SPARSE):
+                nc.vector.tensor_tensor(gated[:], y[group][:], gates[:, s0 : s0 + PIECE], MULT)
+                nc.scalar.activation(window, gated[:], COPY)
+            else:
+                nc.vector.tensor_tensor(window, y[group][:], gates[:, s0 : s0 + PIECE], MULT)
+            left[n] = left[n] - 1
+            if left[n] == 0:
+                nc.sync.dma_start(out=out[P * n : P * (n + 1), :], in_=spread[n][:])

@@ -90,10 +90,13 @@ def tile_moe_rag_lin_silu_kernel(tc, xT, w_words, w_scales, b, gate, offs, out):
         load_x(raw_head, LAST, 0, 2 * PIECE)
         nc.sync.dma_start(out=w_first[:].bitcast(I32), in_=w_words[:, 0].rearrange("e p c -> p e c").bitcast(I32))
         load_x(raw_tail, LAST, 2 * PIECE, T)
-        for e in (1, 0):
+
+        def load_rest(e):
             nc.sync.dma_start(
                 out=w_rest[e][:].bitcast(I32), in_=w_words[e, 1:PASSES].rearrange("a p c -> p a c").bitcast(I32)
             )
+
+        load_rest(1)
 
         def turn_bias_and_gate():
             turned = banks[7]
@@ -160,15 +163,16 @@ def tile_moe_rag_lin_silu_kernel(tc, xT, w_words, w_scales, b, gate, offs, out):
             gather_words(a, EARLY)
             if a == LAST - 1:
                 nc.vector.tensor_copy(slot_planes[0][:], planes[:, 0:WIDE].indirect(entries(0, T)))
-                for moved in range(1, LAST):
+                for moved in (2, 1):
                     row = PLANE_STEP * moved
                     nc.sync.dma_start(
                         out=slot_planes[moved][0:SHIFT_ROWS, :].bitcast(I32),
                         in_=slot_planes[0][row : row + SHIFT_ROWS, :].bitcast(I32),
                     )
-            gather_words(a, SPARSE)
+                load_rest(0)
+            gather_words(a, LATE)
             if a < LAST - 1:
-                gather_words(a, LATE)
+                gather_words(a, SPARSE)
 
         cut = 2 * PIECE - LAST_SHARE
         round_tokens(False, LAST, 0, PIECE)
@@ -177,15 +181,15 @@ def tile_moe_rag_lin_silu_kernel(tc, xT, w_words, w_scales, b, gate, offs, out):
         round_tokens(False, LAST, 2 * PIECE, T)
         quantize(LAST, 0)
         quantize(LAST, PIECE)
-        gather_words(LAST - 1, LATE, over="raw_head")
+        gather_words(LAST - 1, SPARSE, over="raw_head")
         gather_last_plane(EARLY)
         quantize(LAST, 2 * PIECE)
         gather_words(LAST, EARLY, over="raw_tail")
-        for part in (SPARSE, LATE):
+        for part in (LATE, SPARSE):
             gather_words(LAST, part)
             gather_last_plane(part)
 
-        groups = [(2, EARLY), (0, SPARSE), (1, EARLY), (2, SPARSE), (0, EARLY), (2, LATE), (1, LATE), (0, LATE), (1, SPARSE)]
+        groups = [(0, EARLY), (1, EARLY), (2, EARLY), (1, LATE), (0, SPARSE), (2, LATE), (1, SPARSE), (0, LATE), (2, SPARSE)]
         sums = {g: banks[i % 8][:, PIECE * (i // 8) : PIECE * (i // 8 + 1)] for i, g in enumerate(groups)}
         y = {}
 
@@ -221,9 +225,9 @@ def tile_moe_rag_lin_silu_kernel(tc, xT, w_words, w_scales, b, gate, offs, out):
             activate(group)
 
         spread = {
-            0: sbuf("spread0", [P, T], F32, over="bias_sparse_last"),
-            1: sbuf("spread1", [P, T], F32, over="words%d" % LAST),
-            2: sbuf("spread2", [P, T], F32, over="planes"),
+            0: sbuf("spread0", [P, T], F32, over="words%d" % LAST),
+            1: sbuf("spread1", [P, T], F32, over="planes"),
+            2: sbuf("spread2", [P, T], F32),
         }
         left = {n: 3 for n in range(N_BLOCKS)}
         for group in groups:

@@ -50,68 +50,70 @@ def tile_moe_rag_lin_silu_kernel(tc, xT, w_words, w_scales, b, gate, offs, out):
         planes = sbuf("planes", [P, 2 * T], U8)
         slot_words = {}
         slot_planes = [sbuf("slot_planes%d" % a, [P, T], U8) for a in range(PASSES)]
-        w_first = sbuf("w_first", [P, E, 2 * N], U8)
-        w_rest = [sbuf("w_rest%d" % e, [P, LAST, 2 * N], U8) for e in range(E)]
-        w_planes = sbuf("w_planes", [P, E * PASSES, N], U8)
+        w1_first = sbuf("w1_first", [P, 1, 2 * N], U8)
+        w1_rest = sbuf("w1_rest", [P, LAST, 2 * N], U8)
+        w0_codes = sbuf("w0_codes", [P, PASSES, 2 * N], U8)
+        w_planes = [sbuf("w_planes%d" % e, [P, PASSES, N], U8) for e in range(E)]
         bias_rows = sbuf("bias_rows", [P, P * E], F32)
         gate_rows = sbuf("gate_rows", [P, P], F32)
         gate_columns = sbuf("gate_columns", [P, T // P], F32)
         identity = sbuf("identity", [P, P], F32)
         bias_dense = sbuf("bias_dense", [P, N_BLOCKS], F32)
+        bias_sparse_first = sbuf("bias_sparse_first", [P, 1], F32)
         bias_sparse = sbuf("bias_sparse", [P, N_BLOCKS - 1], F32)
-        bias_sparse_last = sbuf("bias_sparse_last", [P, 1], F32)
-        gates = sbuf("gates", [P, T], F32)
         gated = sbuf("gated", [P, PIECE], F32)
         banks = [psum.tile([P, 512], F32, name="bank%d" % i) for i in range(8)]
 
-        nc.vector.memset(w_planes[:].rearrange("p a n -> p (a n)").bitcast(I32), 0)
+        for e in range(E):
+            nc.vector.memset(w_planes[e][:].rearrange("p a n -> p (a n)").bitcast(I32), 0)
         nc.gpsimd.memset(bias_rows[:], 0.0)
         nc.gpsimd.memset(gate_rows[:], 0.0)
         nc.vector.memset(planes[:].bitcast(I32), 0)
         for a in range(1, LAST):
             nc.vector.memset(slot_planes[a][:].bitcast(I32), 0)
         make_identity(nc, identity[:])
-        for r in range(4):
-            nc.gpsimd.dma_start(
-                out=w_planes[r:P:32, :, :].bitcast(I32),
-                in_=w_scales[:, :, r:16:4, :].rearrange("e a q n -> q (e a) n").bitcast(I32),
-            )
 
         def load_x(tile, a, t0, t1):
             rows = xT[a * K_PASS : (a + 1) * K_PASS, t0:t1].rearrange("(p j) t -> p j t", j=PACK)
             nc.sync.dma_start(out=tile[:], in_=rows)
 
+        def load_scales(e):
+            for r in range(4):
+                nc.sync.dma_start(
+                    out=w_planes[e][r:P:32, :, :].bitcast(I32),
+                    in_=w_scales[e, :, r:16:4, :].rearrange("a q n -> q a n").bitcast(I32),
+                )
+
+        def load_codes(tile, e, a0, a1):
+            nc.sync.dma_start(out=tile[:].bitcast(I32), in_=w_words[e, a0:a1].rearrange("a p c -> p a c").bitcast(I32))
+
         load_x(raw[0], 0, 0, T)
         nc.sync.dma_start(offsets[:], offs)
-        nc.sync.dma_start(out=bias_rows[0:N_BLOCKS, :], in_=b.rearrange("(n p) e -> n (p e)", p=P))
-        nc.sync.dma_start(out=gate_rows[0 : T // P, :], in_=gate[0, :].rearrange("(m p) -> m p", p=P))
         load_x(raw[1], 1, 0, T)
         load_x(raw[2], 2, 0, T)
+        nc.sync.dma_start(out=bias_rows[0:N_BLOCKS, :], in_=b.rearrange("(n p) e -> n (p e)", p=P))
+        nc.sync.dma_start(out=gate_rows[0 : T // P, :], in_=gate[0, :].rearrange("(m p) -> m p", p=P))
         load_x(raw_head, LAST, 0, 2 * PIECE)
-        nc.sync.dma_start(out=w_first[:].bitcast(I32), in_=w_words[:, 0].rearrange("e p c -> p e c").bitcast(I32))
+        load_scales(1)
+        load_codes(w1_first, 1, 0, 1)
         load_x(raw_tail, LAST, 2 * PIECE, T)
+        load_codes(w1_rest, 1, 1, PASSES)
 
-        def load_rest(e):
-            nc.sync.dma_start(
-                out=w_rest[e][:].bitcast(I32), in_=w_words[e, 1:PASSES].rearrange("a p c -> p a c").bitcast(I32)
-            )
-
-        load_rest(1)
+        gate_banks = ((banks[6], 0, 2 * PIECE), (banks[7], 2 * PIECE, T))
 
         def turn_bias_and_gate():
-            turned = banks[7]
+            turned = banks[5]
             for e in range(E):
                 nc.tensor.transpose(turned[:, P * e : P * (e + 1)], bias_rows[:, e : E * P : E], identity[:])
             nc.tensor.transpose(turned[:, E * P : (E + 1) * P], gate_rows[:], identity[:])
             nc.scalar.activation(gate_columns[:], turned[:, E * P : E * P + T // P], COPY)
             nc.scalar.activation(bias_dense[:], turned[:, P : P + N_BLOCKS], COPY)
-            nc.scalar.activation(bias_sparse[:], turned[:, 0 : N_BLOCKS - 1], COPY)
-            nc.scalar.activation(bias_sparse_last[:], turned[:, N_BLOCKS - 1 : N_BLOCKS], COPY)
-            for bank, (s0, s1) in ((banks[6], (0, 2 * PIECE)), (banks[5], (2 * PIECE, T))):
+            nc.scalar.activation(bias_sparse_first[:], turned[:, 0:1], COPY)
+            nc.scalar.activation(bias_sparse[:], turned[:, 1:N_BLOCKS], COPY)
+            for bank, s0, s1 in gate_banks:
                 for m in range(s0 // P, s1 // P):
                     column = gate_columns[:, m : m + 1].to_broadcast([P, P])
                     nc.tensor.transpose(bank[:, P * m - s0 : P * (m + 1) - s0], column, identity[:])
-                nc.scalar.activation(gates[:, s0:s1], bank[:, 0 : s1 - s0], COPY)
 
         def round_tokens(on_vector, a, t0, t1):
             if a < LAST:
@@ -152,26 +154,28 @@ def tile_moe_rag_lin_silu_kernel(tc, xT, w_words, w_scales, b, gate, offs, out):
             if a == 0:
                 round_tokens(True, a, PIECE, VECTOR_SHARE[a])
                 round_tokens(False, a, VECTOR_SHARE[a], T)
-                turn_bias_and_gate()
             else:
                 cut = PIECE + VECTOR_SHARE[a]
                 round_tokens(False, a, PIECE, 2 * PIECE)
                 round_tokens(True, a, 2 * PIECE, cut)
                 round_tokens(False, a, cut, T)
+            if a == LAST - 1:
+                turn_bias_and_gate()
             for t0 in range(0, T, PIECE):
                 quantize(a, t0)
             gather_words(a, EARLY)
             if a == LAST - 1:
                 nc.vector.tensor_copy(slot_planes[0][:], planes[:, 0:WIDE].indirect(entries(0, T)))
-                for moved in (2, 1):
+                for moved in range(1, LAST):
                     row = PLANE_STEP * moved
                     nc.sync.dma_start(
                         out=slot_planes[moved][0:SHIFT_ROWS, :].bitcast(I32),
                         in_=slot_planes[0][row : row + SHIFT_ROWS, :].bitcast(I32),
                     )
-                load_rest(0)
-            gather_words(a, LATE)
-            if a < LAST - 1:
+                load_scales(0)
+                load_codes(w0_codes, 0, 0, PASSES)
+            else:
+                gather_words(a, LATE)
                 gather_words(a, SPARSE)
 
         cut = 2 * PIECE - LAST_SHARE
@@ -181,63 +185,87 @@ def tile_moe_rag_lin_silu_kernel(tc, xT, w_words, w_scales, b, gate, offs, out):
         round_tokens(False, LAST, 2 * PIECE, T)
         quantize(LAST, 0)
         quantize(LAST, PIECE)
-        gather_words(LAST - 1, SPARSE, over="raw_head")
+        gather_words(LAST - 1, LATE, over="raw_head")
         gather_last_plane(EARLY)
+        gather_words(LAST, EARLY)
         quantize(LAST, 2 * PIECE)
-        gather_words(LAST, EARLY, over="raw_tail")
+        gather_words(LAST - 1, SPARSE, over="raw_tail")
+        gates = sbuf("gates", [P, T], F32, over="grouped%d" % LAST)
+        for bank, s0, s1 in gate_banks:
+            nc.scalar.activation(gates[:, s0:s1], bank[:, 0 : s1 - s0], COPY)
         for part in (LATE, SPARSE):
             gather_words(LAST, part)
             gather_last_plane(part)
 
-        groups = [(0, EARLY), (1, EARLY), (2, EARLY), (1, LATE), (0, SPARSE), (2, LATE), (1, SPARSE), (0, LATE), (2, SPARSE)]
-        sums = {g: banks[i % 8][:, PIECE * (i // 8) : PIECE * (i // 8 + 1)] for i, g in enumerate(groups)}
+        def sums(n, part):
+            if part == SPARSE:
+                return banks[2 * N_BLOCKS + n % 2][:, PIECE * (n // 2) : PIECE * (n // 2 + 1)]
+            return banks[n if part == EARLY else N_BLOCKS + n][:, 0:PIECE]
+
+        pass_order = {EARLY: (0, 3, 1, 2), LATE: (0, 2, 1, 3), SPARSE: (3, 0, 1, 2)}
         y = {}
 
-        def multiply(a, group):
-            n, (s0, e, columns) = group
-            codes = w_first[:, e, :] if a == 0 else w_rest[e][:, a - 1, :]
+        def multiply(a, n, part):
+            s0, e, columns = part
+            if e == 0:
+                codes = w0_codes[:, a, :]
+            else:
+                codes = w1_first[:, 0, :] if a == 0 else w1_rest[:, a - 1, :]
             nc.tensor.matmul_mx(
-                out=sums[group],
+                out=sums(n, part),
                 lhsT=codes[:, 2 * P * n : 2 * P * (n + 1)].bitcast(E2M1X4),
-                lhsT_scale=w_planes[:, PASSES * e + a, P * n : P * (n + 1)],
-                rhs=slot_words[a, group[1]][:].bitcast(E4M3X4),
+                lhsT_scale=w_planes[e][:, a, P * n : P * (n + 1)],
+                rhs=slot_words[a, part][:].bitcast(E4M3X4),
                 rhs_scale=slot_planes[a][:, s0 : s0 + PIECE],
-                start=(a == 0),
-                stop=(a == LAST),
+                start=(a == pass_order[part][0]),
+                stop=(a == pass_order[part][LAST]),
             )
 
-        def activate(group):
-            n, (s0, e, columns) = group
+        def activate(n, part, over=None):
+            s0, e, columns = part
             if e == 1:
                 bias = bias_dense[:, n : n + 1]
-            elif n < N_BLOCKS - 1:
-                bias = bias_sparse[:, n : n + 1]
             else:
-                bias = bias_sparse_last[:]
-            y[group] = sbuf("y%d_%d" % (n, s0), [P, PIECE], F32)
-            nc.scalar.activation(y[group][:], sums[group], SILU, bias=bias)
+                bias = bias_sparse_first[:] if n == 0 else bias_sparse[:, n - 1 : n]
+            y[n, part] = sbuf("y%d_%d" % (n, s0), [P, PIECE], F32, over)
+            nc.scalar.activation(y[n, part][:], sums(n, part), SILU, bias=bias)
 
-        for group in groups[:8]:
-            multiply(0, group)
-        for i, group in enumerate(groups):
-            for a in range(0 if i == 8 else 1, PASSES):
-                multiply(a, group)
-            activate(group)
+        def finish_group(n, part, first):
+            for a in pass_order[part][first:]:
+                multiply(a, n, part)
+
+        for part in (EARLY, LATE):
+            for n in range(N_BLOCKS):
+                multiply(0, n, part)
+        for a in pass_order[EARLY][1:LAST]:
+            for n in range(N_BLOCKS):
+                multiply(a, n, EARLY)
+        for part, first in ((EARLY, LAST), (LATE, 1)):
+            for n in range(N_BLOCKS):
+                finish_group(n, part, first)
+                if (n, part) != (2, LATE):
+                    activate(n, part)
+        for n in range(N_BLOCKS):
+            finish_group(n, SPARSE, 0)
+            activate(n, SPARSE)
+            if n == 0:
+                activate(2, LATE, over="bias_sparse_first")
 
         spread = {
             0: sbuf("spread0", [P, T], F32, over="words%d" % LAST),
             1: sbuf("spread1", [P, T], F32, over="planes"),
             2: sbuf("spread2", [P, T], F32),
         }
+        scatters = [(0, EARLY), (1, EARLY), (2, EARLY), (1, LATE), (0, SPARSE), (2, LATE), (1, SPARSE), (0, LATE), (2, SPARSE)]
         left = {n: 3 for n in range(N_BLOCKS)}
-        for group in groups:
-            n, (s0, e, columns) = group
+        for n, part in scatters:
+            s0, e, columns = part
             window = spread[n][:].indirect(entries(s0))
-            if group == (0, SPARSE):
-                nc.vector.tensor_tensor(gated[:], y[group][:], gates[:, s0 : s0 + PIECE], MULT)
+            if (n, part) == (0, SPARSE):
+                nc.vector.tensor_tensor(gated[:], y[n, part][:], gates[:, s0 : s0 + PIECE], MULT)
                 nc.scalar.activation(window, gated[:], COPY)
             else:
-                nc.vector.tensor_tensor(window, y[group][:], gates[:, s0 : s0 + PIECE], MULT)
+                nc.vector.tensor_tensor(window, y[n, part][:], gates[:, s0 : s0 + PIECE], MULT)
             left[n] = left[n] - 1
             if left[n] == 0:
                 nc.sync.dma_start(out=out[P * n : P * (n + 1), :], in_=spread[n][:])

@@ -61,6 +61,7 @@ def tile_moe_rag_lin_silu_kernel(tc, xT, w_words, w_scales, b, gate, offs, out):
         bias_dense = sbuf("bias_dense", [P, N_BLOCKS], F32)
         bias_sparse_first = sbuf("bias_sparse_first", [P, 1], F32)
         bias_sparse = sbuf("bias_sparse", [P, N_BLOCKS - 1], F32)
+        gates = sbuf("gates", [P, T], F32)
         gated = sbuf("gated", [P, PIECE], F32)
         banks = [psum.tile([P, 512], F32, name="bank%d" % i) for i in range(8)]
 
@@ -89,10 +90,10 @@ def tile_moe_rag_lin_silu_kernel(tc, xT, w_words, w_scales, b, gate, offs, out):
 
         load_x(raw[0], 0, 0, T)
         nc.sync.dma_start(offsets[:], offs)
-        load_x(raw[1], 1, 0, T)
-        load_x(raw[2], 2, 0, T)
         nc.sync.dma_start(out=bias_rows[0:N_BLOCKS, :], in_=b.rearrange("(n p) e -> n (p e)", p=P))
         nc.sync.dma_start(out=gate_rows[0 : T // P, :], in_=gate[0, :].rearrange("(m p) -> m p", p=P))
+        load_x(raw[1], 1, 0, T)
+        load_x(raw[2], 2, 0, T)
         load_x(raw_head, LAST, 0, 2 * PIECE)
         load_scales(1)
         load_codes(w1_first, 1, 0, 1)
@@ -114,6 +115,7 @@ def tile_moe_rag_lin_silu_kernel(tc, xT, w_words, w_scales, b, gate, offs, out):
                 for m in range(s0 // P, s1 // P):
                     column = gate_columns[:, m : m + 1].to_broadcast([P, P])
                     nc.tensor.transpose(bank[:, P * m - s0 : P * (m + 1) - s0], column, identity[:])
+                nc.scalar.activation(gates[:, s0:s1], bank[:, 0 : s1 - s0], COPY)
 
         def round_tokens(on_vector, a, t0, t1):
             if a < LAST:
@@ -159,7 +161,7 @@ def tile_moe_rag_lin_silu_kernel(tc, xT, w_words, w_scales, b, gate, offs, out):
                 round_tokens(False, a, PIECE, 2 * PIECE)
                 round_tokens(True, a, 2 * PIECE, cut)
                 round_tokens(False, a, cut, T)
-            if a == LAST - 1:
+            if a == 0:
                 turn_bias_and_gate()
             for t0 in range(0, T, PIECE):
                 quantize(a, t0)
@@ -190,9 +192,6 @@ def tile_moe_rag_lin_silu_kernel(tc, xT, w_words, w_scales, b, gate, offs, out):
         gather_words(LAST, EARLY)
         quantize(LAST, 2 * PIECE)
         gather_words(LAST - 1, SPARSE, over="raw_tail")
-        gates = sbuf("gates", [P, T], F32, over="grouped%d" % LAST)
-        for bank, s0, s1 in gate_banks:
-            nc.scalar.activation(gates[:, s0:s1], bank[:, 0 : s1 - s0], COPY)
         for part in (LATE, SPARSE):
             gather_words(LAST, part)
             gather_last_plane(part)

@@ -58,11 +58,11 @@ def tile_moe_rag_lin_silu_kernel(tc, xT, w_words, w_scales, b, gate, offs, out):
         gate_rows = sbuf("gate_rows", [P, P], F32)
         gate_columns = sbuf("gate_columns", [P, T // P], F32)
         identity = sbuf("identity", [P, P], F32)
-        bias_dense = sbuf("bias_dense", [P, N_BLOCKS], F32)
+        bias_dense = sbuf("bias_dense", [P, N_BLOCKS - 1], F32)
+        bias_dense_middle = sbuf("bias_dense_middle", [P, 1], F32)
         bias_sparse_first = sbuf("bias_sparse_first", [P, 1], F32)
         bias_sparse = sbuf("bias_sparse", [P, N_BLOCKS - 1], F32)
         gates = sbuf("gates", [P, T], F32)
-        gated = sbuf("gated", [P, PIECE], F32)
         banks = [psum.tile([P, 512], F32, name="bank%d" % i) for i in range(8)]
 
         for e in range(E):
@@ -108,7 +108,8 @@ def tile_moe_rag_lin_silu_kernel(tc, xT, w_words, w_scales, b, gate, offs, out):
                 nc.tensor.transpose(turned[:, P * e : P * (e + 1)], bias_rows[:, e : E * P : E], identity[:])
             nc.tensor.transpose(turned[:, E * P : (E + 1) * P], gate_rows[:], identity[:])
             nc.scalar.activation(gate_columns[:], turned[:, E * P : E * P + T // P], COPY)
-            nc.scalar.activation(bias_dense[:], turned[:, P : P + N_BLOCKS], COPY)
+            nc.scalar.activation(bias_dense[:], turned[:, P : P + N_BLOCKS : 2], COPY)
+            nc.scalar.activation(bias_dense_middle[:], turned[:, P + 1 : P + 2], COPY)
             nc.scalar.activation(bias_sparse_first[:], turned[:, 0:1], COPY)
             nc.scalar.activation(bias_sparse[:], turned[:, 1:N_BLOCKS], COPY)
             for bank, s0, s1 in gate_banks:
@@ -223,7 +224,7 @@ def tile_moe_rag_lin_silu_kernel(tc, xT, w_words, w_scales, b, gate, offs, out):
         def activate(n, part, over=None):
             s0, e, columns = part
             if e == 1:
-                bias = bias_dense[:, n : n + 1]
+                bias = bias_dense_middle[:] if n == 1 else bias_dense[:, n // 2 : n // 2 + 1]
             else:
                 bias = bias_sparse_first[:] if n == 0 else bias_sparse[:, n - 1 : n]
             y[n, part] = sbuf("y%d_%d" % (n, s0), [P, PIECE], F32, over)
@@ -239,32 +240,48 @@ def tile_moe_rag_lin_silu_kernel(tc, xT, w_words, w_scales, b, gate, offs, out):
         for a in pass_order[EARLY][1:LAST]:
             for n in range(N_BLOCKS):
                 multiply(a, n, EARLY)
-        for part, first in ((EARLY, LAST), (LATE, 1)):
-            for n in range(N_BLOCKS):
-                finish_group(n, part, first)
-                if (n, part) != (2, LATE):
-                    activate(n, part)
+        spread = {}
+
+        def scatter(n, part):
+            s0, e, columns = part
+            window = spread[n][:].indirect(entries(s0))
+            nc.vector.tensor_tensor(window, y[n, part][:], gates[:, s0 : s0 + PIECE], MULT)
+
+        def scatter_on_scalar(n, part, over=None):
+            s0, e, columns = part
+            gated = sbuf("gated%d" % s0, [P, PIECE], F32, over)
+            nc.vector.tensor_tensor(gated[:], y[n, part][:], gates[:, s0 : s0 + PIECE], MULT)
+            nc.scalar.activation(spread[n][:].indirect(entries(s0)), gated[:], COPY)
+
+        def store(n):
+            nc.sync.dma_start(out=out[P * n : P * (n + 1), :], in_=spread[n][:])
+
+        for n in range(N_BLOCKS):
+            finish_group(n, EARLY, LAST)
+            activate(n, EARLY)
+        finish_group(1, LATE, 1)
+        activate(1, LATE)
+        spread[0] = sbuf("spread0", [P, T], F32, over="bias_dense_middle")
+        spread[1] = sbuf("spread1", [P, T], F32, over="planes")
+        spread[2] = sbuf("spread2", [P, T], F32)
+        scatter_on_scalar(0, EARLY, over="words%d" % LAST)
+        finish_group(0, LATE, 1)
+        activate(0, LATE)
+        finish_group(2, LATE, 1)
         for n in range(N_BLOCKS):
             finish_group(n, SPARSE, 0)
             activate(n, SPARSE)
             if n == 0:
                 activate(2, LATE, over="bias_sparse_first")
 
-        spread = {
-            0: sbuf("spread0", [P, T], F32, over="words%d" % LAST),
-            1: sbuf("spread1", [P, T], F32, over="planes"),
-            2: sbuf("spread2", [P, T], F32),
-        }
-        scatters = [(0, EARLY), (1, EARLY), (2, EARLY), (1, LATE), (0, SPARSE), (2, LATE), (1, SPARSE), (0, LATE), (2, SPARSE)]
-        left = {n: 3 for n in range(N_BLOCKS)}
-        for n, part in scatters:
-            s0, e, columns = part
-            window = spread[n][:].indirect(entries(s0))
-            if (n, part) == (0, SPARSE):
-                nc.vector.tensor_tensor(gated[:], y[n, part][:], gates[:, s0 : s0 + PIECE], MULT)
-                nc.scalar.activation(window, gated[:], COPY)
-            else:
-                nc.vector.tensor_tensor(window, y[n, part][:], gates[:, s0 : s0 + PIECE], MULT)
-            left[n] = left[n] - 1
-            if left[n] == 0:
-                nc.sync.dma_start(out=out[P * n : P * (n + 1), :], in_=spread[n][:])
+        scatter(1, EARLY)
+        scatter(2, EARLY)
+        scatter(1, LATE)
+        scatter_on_scalar(0, SPARSE)
+        scatter(2, LATE)
+        scatter(1, SPARSE)
+        store(1)
+        scatter(0, LATE)
+        store(0)
+        scatter(2, SPARSE)
+        store(2)

import concourse.mybir as mybir
from concourse.masks import make_identity

K, T, E, N = 2048, 768, 2, 384
FLOPS = 2 * T * K * N
BYTES = 4 * K * T + E * K * N // 2 + E * K * N // 32 + 4 * N * E + 4 * T + 2 * T + 4 * N * T

P = 128
PACK = 4
K_PASS = P * PACK
PASSES = K // K_PASS
LAST = PASSES - 1
N_BLOCKS = N // P
PIECE = 256
WIDE = 1024
PLANE_STEP = 4
SHIFT_ROWS = 112
RUN = 4
VECTOR_SHARE = (512, 416, 416)
LAST_SHARE = 128

EARLY, LATE, SPARSE = (256, 1, 2 * PIECE), (512, 1, T), (0, 0, T)

F32 = mybir.dt.float32
BF16 = mybir.dt.bfloat16
I32 = mybir.dt.int32
U32 = mybir.dt.uint32
U16 = mybir.dt.uint16
U8 = mybir.dt.uint8
E4M3X4 = mybir.dt.float8_e4m3fn_x4
E2M1X4 = mybir.dt.float4_e2m1fn_x4
COPY = mybir.ActivationFunctionType.Copy
SILU = mybir.ActivationFunctionType.Silu
MULT = mybir.AluOpType.mult


def tile_moe_rag_lin_silu_kernel(tc, xT, w_words, w_scales, b, gate, offs, out):
    nc = tc.nc
    with tc.tile_pool(name="keep", bufs=1) as keep, tc.psum_pool(name="psum", bufs=1) as psum:

        def sbuf(name, shape, dtype, over=None):
            return keep.tile(shape, dtype, name=name, tag=over or name, align_bytes=64)

        offsets = keep.tile([P, T // 16], U16, name="offsets")
        raw = [sbuf("raw%d" % a, [P, PACK, T], F32) for a in range(LAST)]
        raw_head = sbuf("raw_head", [P, PACK, 2 * PIECE], F32)
        raw_tail = sbuf("raw_tail", [P, PACK, PIECE], F32)
        grouped = [sbuf("grouped%d" % a, [P, T, PACK], BF16) for a in range(PASSES)]
        words = [sbuf("words%d" % a, [P, T], I32) for a in range(PASSES)]
        planes = sbuf("planes", [P, 2 * T], U8)
        slot_words = {}
        slot_planes = [sbuf("slot_planes%d" % a, [P, T], U8) for a in range(PASSES)]
        w1_first = sbuf("w1_first", [P, 1, 2 * N], U8)
        w1_rest = sbuf("w1_rest", [P, LAST, 2 * N], U8)
        w0_codes = sbuf("w0_codes", [P, PASSES, 2 * N], U8)
        w_planes = [sbuf("w_planes%d" % e, [P, PASSES, N], U8) for e in range(E)]
        bias_rows = sbuf("bias_rows", [P, P * E], F32)
        gate_rows = sbuf("gate_rows", [P, P], F32)
        gate_columns = sbuf("gate_columns", [P, T // P], F32)
        identity = sbuf("identity", [P, P], F32)
        bias_dense = sbuf("bias_dense", [P, N_BLOCKS - 1], F32)
        bias_dense_middle = sbuf("bias_dense_middle", [P, 1], F32)
        bias_sparse_first = sbuf("bias_sparse_first", [P, 1], F32)
        bias_sparse = sbuf("bias_sparse", [P, N_BLOCKS - 1], F32)
        gates = sbuf("gates", [P, T], F32)
        banks = [psum.tile([P, 512], F32, name="bank%d" % i) for i in range(8)]

        for e in range(E):
            nc.vector.memset(w_planes[e][:].rearrange("p a n -> p (a n)").bitcast(I32), 0)
        nc.gpsimd.memset(bias_rows[:], 0.0)
        nc.gpsimd.memset(gate_rows[:], 0.0)
        nc.vector.memset(planes[:].bitcast(I32), 0)
        for a in range(1, LAST):
            nc.vector.memset(slot_planes[a][:].bitcast(I32), 0)
        make_identity(nc, identity[:])

        def load_x(tile, a, t0, t1):
            rows = xT[a * K_PASS : (a + 1) * K_PASS, t0:t1].rearrange("(p j) t -> p j t", j=PACK)
            nc.sync.dma_start(out=tile[:], in_=rows)

        def load_scales(e):
            for r in range(4):
                nc.sync.dma_start(
                    out=w_planes[e][r:P:32, :, :].bitcast(I32),
                    in_=w_scales[e, :, r:16:4, :].rearrange("a q n -> q a n").bitcast(I32),
                )

        def load_codes(tile, e, a0, a1):
            nc.sync.dma_start(out=tile[:].bitcast(I32), in_=w_words[e, a0:a1].rearrange("a p c -> p a c").bitcast(I32))

        load_x(raw[0], 0, 0, T)
        nc.sync.dma_start(offsets[:], offs)
        nc.sync.dma_start(out=bias_rows[0:N_BLOCKS, :], in_=b.rearrange("(n p) e -> n (p e)", p=P))
        nc.sync.dma_start(out=gate_rows[0 : T // P, :], in_=gate[0, :].rearrange("(m p) -> m p", p=P))
        load_x(raw[1], 1, 0, T)
        load_x(raw[2], 2, 0, T)
        load_x(raw_head, LAST, 0, 2 * PIECE)
        load_scales(1)
        load_codes(w1_first, 1, 0, 1)
        load_x(raw_tail, LAST, 2 * PIECE, T)
        load_codes(w1_rest, 1, 1, PASSES)

        gate_banks = ((banks[6], 0, 2 * PIECE), (banks[7], 2 * PIECE, T))

        def turn_bias_and_gate():
            turned = banks[5]
            for e in range(E):
                nc.tensor.transpose(turned[:, P * e : P * (e + 1)], bias_rows[:, e : E * P : E], identity[:])
            nc.tensor.transpose(turned[:, E * P : (E + 1) * P], gate_rows[:], identity[:])
            nc.scalar.activation(gate_columns[:], turned[:, E * P : E * P + T // P], COPY)
            nc.scalar.activation(bias_dense[:], turned[:, P : P + N_BLOCKS : 2], COPY)
            nc.scalar.activation(bias_dense_middle[:], turned[:, P + 1 : P + 2], COPY)
            nc.scalar.activation(bias_sparse_first[:], turned[:, 0:1], COPY)
            nc.scalar.activation(bias_sparse[:], turned[:, 1:N_BLOCKS], COPY)
            for bank, s0, s1 in gate_banks:
                for m in range(s0 // P, s1 // P):
                    column = gate_columns[:, m : m + 1].to_broadcast([P, P])
                    nc.tensor.transpose(bank[:, P * m - s0 : P * (m + 1) - s0], column, identity[:])
                nc.scalar.activation(gates[:, s0:s1], bank[:, 0 : s1 - s0], COPY)

        def round_tokens(on_vector, a, t0, t1):
            if a < LAST:
                src = raw[a][:, :, t0:t1]
            elif t1 <= 2 * PIECE:
                src = raw_head[:, :, t0:t1]
            else:
                src = raw_tail[:, :, t0 - 2 * PIECE : t1 - 2 * PIECE]
            src = src.rearrange("p j (c i) -> p c j i", i=RUN)
            dst = grouped[a][:, t0:t1, :].rearrange("p (c i) j -> p c j i", i=RUN)
            if on_vector:
                nc.vector.tensor_copy(dst, src)
            else:
                nc.scalar.activation(dst, src, COPY)

        def quantize(a, t0):
            row, column = (0, T + t0) if a == LAST else (PLANE_STEP * a, t0)
            nc.vector.quantize_mx(
                out=words[a][:, t0 : t0 + PIECE].bitcast(E4M3X4),
                scales=planes[row:P, column : column + PIECE],
                in_=grouped[a][:, t0 : t0 + PIECE, :].rearrange("p t j -> p (t j)"),
            )

        def entries(s0, count=PIECE):
            return offsets[:, s0 // 16 : (s0 + count) // 16]

        def gather_words(a, part, over=None):
            s0, e, columns = part
            slot_words[a, part] = sbuf("slot_words%d_%d" % (a, s0), [P, PIECE], U32, over)
            nc.vector.tensor_copy(slot_words[a, part][:], words[a][:, 0:columns].bitcast(U32).indirect(entries(s0)))

        def gather_last_plane(part):
            s0, e, columns = part
            nc.vector.tensor_copy(slot_planes[LAST][:, s0 : s0 + PIECE], planes[:, T : T + columns].indirect(entries(s0)))

        for a in range(LAST):
            round_tokens(True, a, 0, PIECE)
            if a == 0:
                round_tokens(True, a, PIECE, VECTOR_SHARE[a])
                round_tokens(False, a, VECTOR_SHARE[a], T)
            else:
                cut = PIECE + VECTOR_SHARE[a]
                round_tokens(False, a, PIECE, 2 * PIECE)
                round_tokens(True, a, 2 * PIECE, cut)
                round_tokens(False, a, cut, T)
            if a == 0:
                turn_bias_and_gate()
            for t0 in range(0, T, PIECE):
                quantize(a, t0)
            gather_words(a, EARLY)
            if a == LAST - 1:
                nc.vector.tensor_copy(slot_planes[0][:], planes[:, 0:WIDE].indirect(entries(0, T)))
                for moved in range(1, LAST):
                    row = PLANE_STEP * moved
                    nc.sync.dma_start(
                        out=slot_planes[moved][0:SHIFT_ROWS, :].bitcast(I32),
                        in_=slot_planes[0][row : row + SHIFT_ROWS, :].bitcast(I32),
                    )
                load_scales(0)
                load_codes(w0_codes, 0, 0, PASSES)
            else:
                gather_words(a, LATE)
                gather_words(a, SPARSE)

        cut = 2 * PIECE - LAST_SHARE
        round_tokens(False, LAST, 0, PIECE)
        round_tokens(False, LAST, PIECE, cut)
        round_tokens(True, LAST, cut, 2 * PIECE)
        round_tokens(False, LAST, 2 * PIECE, T)
        quantize(LAST, 0)
        quantize(LAST, PIECE)
        gather_words(LAST - 1, LATE, over="raw_head")
        gather_last_plane(EARLY)
        gather_words(LAST, EARLY)
        quantize(LAST, 2 * PIECE)
        gather_words(LAST - 1, SPARSE, over="raw_tail")
        for part in (LATE, SPARSE):
            gather_words(LAST, part)
            gather_last_plane(part)

        def sums(n, part):
            if part == SPARSE:
                return banks[2 * N_BLOCKS + n % 2][:, PIECE * (n // 2) : PIECE * (n // 2 + 1)]
            return banks[n if part == EARLY else N_BLOCKS + n][:, 0:PIECE]

        pass_order = {EARLY: (0, 3, 1, 2), LATE: (0, 2, 1, 3), SPARSE: (3, 0, 1, 2)}
        y = {}

        def multiply(a, n, part):
            s0, e, columns = part
            if e == 0:
                codes = w0_codes[:, a, :]
            else:
                codes = w1_first[:, 0, :] if a == 0 else w1_rest[:, a - 1, :]
            nc.tensor.matmul_mx(
                out=sums(n, part),
                lhsT=codes[:, 2 * P * n : 2 * P * (n + 1)].bitcast(E2M1X4),
                lhsT_scale=w_planes[e][:, a, P * n : P * (n + 1)],
                rhs=slot_words[a, part][:].bitcast(E4M3X4),
                rhs_scale=slot_planes[a][:, s0 : s0 + PIECE],
                start=(a == pass_order[part][0]),
                stop=(a == pass_order[part][LAST]),
            )

        def activate(n, part, over=None):
            s0, e, columns = part
            if e == 1:
                bias = bias_dense_middle[:] if n == 1 else bias_dense[:, n // 2 : n // 2 + 1]
            else:
                bias = bias_sparse_first[:] if n == 0 else bias_sparse[:, n - 1 : n]
            y[n, part] = sbuf("y%d_%d" % (n, s0), [P, PIECE], F32, over)
            nc.scalar.activation(y[n, part][:], sums(n, part), SILU, bias=bias)

        def finish_group(n, part, first):
            for a in pass_order[part][first:]:
                multiply(a, n, part)

        for part in (EARLY, LATE):
            for n in range(N_BLOCKS):
                multiply(0, n, part)
        for a in pass_order[EARLY][1:LAST]:
            for n in range(N_BLOCKS):
                multiply(a, n, EARLY)
        spread = {}

        def scatter(n, part):
            s0, e, columns = part
            window = spread[n][:].indirect(entries(s0))
            nc.vector.tensor_tensor(window, y[n, part][:], gates[:, s0 : s0 + PIECE], MULT)

        def scatter_on_scalar(n, part, over=None):
            s0, e, columns = part
            gated = sbuf("gated%d" % s0, [P, PIECE], F32, over)
            nc.vector.tensor_tensor(gated[:], y[n, part][:], gates[:, s0 : s0 + PIECE], MULT)
            nc.scalar.activation(spread[n][:].indirect(entries(s0)), gated[:], COPY)

        def store(n):
            nc.sync.dma_start(out=out[P * n : P * (n + 1), :], in_=spread[n][:])

        for n in range(N_BLOCKS):
            finish_group(n, EARLY, LAST)
            activate(n, EARLY)
        finish_group(1, LATE, 1)
        activate(1, LATE)
        spread[0] = sbuf("spread0", [P, T], F32, over="bias_dense_middle")
        spread[1] = sbuf("spread1", [P, T], F32, over="planes")
        spread[2] = sbuf("spread2", [P, T], F32)
        scatter_on_scalar(0, EARLY, over="words%d" % LAST)
        finish_group(0, LATE, 1)
        activate(0, LATE)
        finish_group(2, LATE, 1)
        for n in range(N_BLOCKS):
            finish_group(n, SPARSE, 0)
            activate(n, SPARSE)
            if n == 0:
                activate(2, LATE, over="bias_sparse_first")

        scatter(1, EARLY)
        scatter(2, EARLY)
        scatter(1, LATE)
        scatter_on_scalar(0, SPARSE)
        scatter(2, LATE)
        scatter(1, SPARSE)
        store(1)
        scatter(0, LATE)
        store(0)
        scatter(2, SPARSE)
        store(2)
